import numpy as np
import ml_dtypes


def mxq(x, axis, fmt="e4m3"):
    dtype, down = {"e4m3": (ml_dtypes.float8_e4m3fn, 7), "e5m2": (ml_dtypes.float8_e5m2, 14)}[fmt]
    v = np.moveaxis(np.asarray(x, np.float32).astype(ml_dtypes.bfloat16).astype(np.float64), axis, -1)
    blocks = v.reshape(v.shape[:-1] + (-1, 32))
    amax = np.abs(blocks).max(-1, keepdims=True)
    byte = np.maximum(np.where(amax > 0, np.frexp(amax)[1] - 1 + 127, 0) - down, 1)
    scale = np.exp2(byte - 127.0)
    codes = (blocks / scale).astype(np.float32).astype(dtype).astype(np.float64)
    return np.moveaxis((codes * scale).reshape(v.shape), -1, axis)


WIDE = False


def mx_kscale(k):
    if not WIDE:
        return np.ones(k)
    levels = np.array([10, -10, 5, -5, 0])
    if k % 512:
        return np.exp2(np.random.permutation(np.resize(levels, k // 32))).repeat(32)
    a = np.empty((k // 512, 16))
    for p in range(k // 512):
        a[p, :8] = np.random.permutation(np.resize(levels, 8))
        for g in range(8):
            far = levels[np.abs(levels - a[p, g]) >= 10]
            a[p, g + 8] = far[np.random.randint(len(far))]
    return np.exp2(a.ravel()).repeat(32)


def f64(x):
    return np.asarray(x).astype(np.float64)


def striped8(idx):
    return np.concatenate([x.reshape(-1, 16).T for x in idx]).astype(np.uint16)


def runs(offs, k):
    lists = np.stack([offs[16 * r : 16 * r + 16].T.reshape(-1) for r in range(8)]).astype(np.int64)
    return lists[np.arange(k) % 512 // 64]


def pack_weight(w):
    k, n = w.shape
    w = f64(np.asarray(w, np.float32).astype(ml_dtypes.bfloat16)).reshape(k // 32, 32, n)
    amax = np.abs(w).max(1)
    byte = np.clip(np.where(amax > 0, np.frexp(amax)[1] - 1 + 127 - 7, 1), 1, 254)
    scaled = (w * np.exp2(127.0 - byte)[:, None, :]).reshape(k, n).astype(np.float32)
    words = np.ascontiguousarray(scaled.reshape(k // 512, 128, 4, n).transpose(0, 1, 3, 2)).astype(ml_dtypes.float8_e4m3fn).view(np.uint8)
    return words, np.ascontiguousarray(byte.astype(np.uint8).reshape(k // 512, 16, n))


def unpack_weight(words, scales):
    g, p, n, _ = words.shape
    vals = np.ascontiguousarray(words).view(ml_dtypes.float8_e4m3fn).astype(np.float64) * np.repeat(np.exp2(scales.astype(np.float64) - 127.0), 8, axis=1)[..., None]
    return vals.transpose(0, 1, 3, 2).reshape(g * 512, n)


E2M1 = np.array([0.0, 0.5, 1.0, 1.5, 2.0, 3.0, 4.0, 6.0, -0.0, -0.5, -1.0, -1.5, -2.0, -3.0, -4.0, -6.0])


def pack_fp4(w):
    k, n = w.shape
    w = f64(np.asarray(w, np.float32).astype(ml_dtypes.bfloat16)).reshape(k // 32, 32, n)
    amax = np.abs(w).max(1)
    mant, ex = np.frexp(amax / 6.0)
    byte = np.clip(np.where(amax > 0, np.where(mant > 0.5, ex, ex - 1) + 127, 1), 1, 254)
    scaled = (w * np.exp2(127.0 - byte)[:, None, :]).reshape(k, n).astype(np.float32)
    c = np.ascontiguousarray(scaled.reshape(k // 512, 128, 4, n).transpose(0, 1, 3, 2)).astype(ml_dtypes.float4_e2m1fn).view(np.uint8) & 0xF
    words = (c[..., 0::2] | (c[..., 1::2] << 4)).reshape(k // 512, 128, 2 * n)
    return np.ascontiguousarray(words), np.ascontiguousarray(byte.astype(np.uint8).reshape(k // 512, 16, n))


def unpack_fp4(words, scales):
    g, _, n = scales.shape
    words = np.ascontiguousarray(words).reshape(g, 128, n, 2)
    nib = np.empty((g, 128, n, 4), np.uint8)
    nib[..., 0::2] = words & 0xF
    nib[..., 1::2] = words >> 4
    vals = E2M1[nib] * np.repeat(np.exp2(scales.astype(np.float64) - 127.0), 8, axis=1)[..., None]
    return vals.transpose(0, 1, 3, 2).reshape(g * 512, n)


K, T, S, H, N = 1024, 2048, 512, 512, 256


def setup_inputs():
    n = np.random.standard_normal
    s = mx_kscale(K)[:, None]
    u = mx_kscale(H)
    packed_xT = pack_weight(n((K, T)) * s)
    packed_w1 = pack_fp4(n((K, N)) / np.sqrt(2 * K) / s)
    packed_w3 = pack_fp4(n((H, N)) / np.sqrt(2 * H) / u[:, None])
    return {
        "x_words": packed_xT[0],
        "x_scales": packed_xT[1],
        "w1_words": packed_w1[0],
        "w1_scales": packed_w1[1],
        "w2": (n((K, H)) / np.sqrt(K) / s * u).astype(np.float32),
        "w3_words": packed_w3[0],
        "w3_scales": packed_w3[1],
        "offs": striped8(np.stack([np.random.permutation(T)[:S] for _ in range(8)])),
    }


def reference(x_words, x_scales, w1_words, w1_scales, w2, w3_words, w3_scales, offs):
    xq = unpack_weight(x_words, x_scales)[np.arange(K)[:, None], runs(offs, K)]
    h = mxq(f64(w2), 0, "e4m3").T @ xq
    return unpack_fp4(w1_words, w1_scales).T @ xq + unpack_fp4(w3_words, w3_scales).T @ mxq(h, 0, "e4m3")

@@ -1,0 +1,206 @@
+from contextlib import ExitStack
+
+import concourse.mybir as mybir
+
+K, T, S, H, N = 1024, 2048, 512, 512, 256
+FLOPS = 2 * S * (K * H + K * N + H * N)
+
+F32 = mybir.dt.float32
+BF16 = mybir.dt.bfloat16
+I32 = mybir.dt.int32
+U32 = mybir.dt.uint32
+U16 = mybir.dt.uint16
+U8 = mybir.dt.uint8
+FP8X4 = mybir.dt.float8_e4m3fn_x4
+FP4X4 = mybir.dt.float4_e2m1fn_x4
+
+P = 128
+PACK = 4
+K_PASS = P * PACK
+PASSES = K // K_PASS
+CHUNK = 128
+CHUNKS = S // CHUNK
+GATHER = 256
+M_TILES = N // P
+HALF = P // 2
+SCALAR_SHARE = 24
+
+
+def tile_picked_phlora_none_p_kernel(
+    tc, x_words, x_scales, w1_words, w1_scales, w2, w3_words, w3_scales, offs, out
+):
+    nc = tc.nc
+    with ExitStack() as ctx:
+        sb = ctx.enter_context(tc.tile_pool(name="sb", bufs=1))
+        ps = ctx.enter_context(tc.psum_pool(name="ps", bufs=1))
+
+        offsets = sb.tile([P, S // 16], U16, name="offsets")
+        nc.sync.dma_start(offsets[:], offs)
+
+        byte_window = sb.tile([P, T], U8, name="byte_window", align_bytes=64)
+        nc.gpsimd.memset(byte_window[:].bitcast(I32), 0)
+        nc.scalar.dma_start(
+            byte_window[0:P:4, :].bitcast(I32), x_scales.rearrange("z q c -> q z c").bitcast(I32)
+        )
+        warm_in = sb.tile([P, 1], F32, name="warm_in")
+        warm_out = sb.tile([P, 1], F32, name="warm_out")
+        nc.gpsimd.memset(warm_in[:], 0.0)
+        nc.scalar.copy(warm_out[:], warm_in[:])
+        x_plane = sb.tile([P, PASSES * S], U8, name="x_plane", align_bytes=64)
+        nc.vector.memset(x_plane[:].bitcast(I32), 0)
+
+        w1_codes = sb.tile([P, PASSES, 2 * N], U8, name="w1_codes", align_bytes=64)
+        nc.sync.dma_start(w1_codes[:].bitcast(I32), w1_words.rearrange("z p b -> p z b").bitcast(I32))
+        w3_codes = sb.tile([P, 2 * N], U8, name="w3_codes", align_bytes=64)
+        nc.sync.dma_start(w3_codes[:].bitcast(I32), w3_words[0].bitcast(I32))
+
+        w1_plane = sb.tile([P, PASSES, N], U8, name="w1_plane", align_bytes=64)
+        w3_plane = sb.tile([P, N], U8, name="w3_plane", align_bytes=64)
+        nc.vector.memset(w1_plane[:].bitcast(I32), 0)
+        nc.vector.memset(w3_plane[:].bitcast(I32), 0)
+        for q in range(4):
+            nc.gpsimd.dma_start(
+                w1_plane[32 * q : 32 * q + 4, :, :].bitcast(I32),
+                w1_scales[:, 4 * q : 4 * q + 4, :].rearrange("z r n -> r z n").bitcast(I32),
+            )
+        for q in range(4):
+            nc.gpsimd.dma_start(
+                w3_plane[32 * q : 32 * q + 4, :].bitcast(I32),
+                w3_scales[0, 4 * q : 4 * q + 4, :].bitcast(I32),
+            )
+
+        w2_first = sb.tile([P, PACK, H], F32, name="w2_first")
+        nc.sync.dma_start(w2_first[:], w2[0:K_PASS, :].rearrange("(p j) c -> p j c", j=PACK))
+        word_window = [sb.tile([P, T], I32, name="word_window%d" % z) for z in range(PASSES)]
+        for z in range(PASSES):
+            nc.sync.dma_start(word_window[z][:], x_words[z].rearrange("p c r -> p (c r)").bitcast(I32))
+
+        def load_w2_last(u, tag):
+            raw = sb.tile([P, PACK, H // 2], F32, name="w2_last%d" % u, tag=tag, align_bytes=64)
+            nc.sync.dma_start(
+                raw[:], w2[K_PASS:K, u * H // 2 : (u + 1) * H // 2].rearrange("(p j) c -> p j c", j=PACK)
+            )
+            return raw
+
+        w2_last = [load_w2_last(0, "w2_last0")]
+
+        picked_bytes = sb.tile([P, S], U8, name="picked_bytes", tag="after_moves", align_bytes=64)
+        nc.vector.tensor_copy(picked_bytes[:], byte_window[:].indirect(offsets[:]))
+        for q in range(4):
+            nc.scalar.dma_start(
+                x_plane[32 * q : 32 * q + 4, :].bitcast(I32).rearrange("p (z s) -> p z s", z=PASSES),
+                picked_bytes[32 * q : 32 * q + 32 : 4, :].bitcast(I32),
+            )
+
+        w2_last.append(load_w2_last(1, "after_moves"))
+
+        w2_codes = [sb.tile([P, H], U32, name="w2_codes%d" % z, align_bytes=64) for z in range(PASSES)]
+        w2_plane = [sb.tile([P, H], U8, name="w2_plane%d" % z, align_bytes=64) for z in range(PASSES)]
+
+        def deal(copy, grouped, raw, m0, m1):
+            copy(
+                grouped[:, :, m0:m1, :].rearrange("p t m j -> p m j t"),
+                raw[:].rearrange("p j (m t) -> p m j t", t=PACK)[:, m0:m1, :, :],
+            )
+
+        grouped_first = sb.tile([P, PACK, P, PACK], BF16, name="grouped_first", align_bytes=64)
+        deal(nc.scalar.copy, grouped_first, w2_first, 0, P)
+        nc.vector.quantize_mx(
+            out=w2_codes[0][:].bitcast(FP8X4),
+            scales=w2_plane[0][:],
+            in_=grouped_first[:].rearrange("p t m j -> p (t m j)"),
+        )
+
+        x_codes = [sb.tile([P, S], U32, name="x_codes%d" % z, align_bytes=64) for z in range(PASSES)]
+
+        def gather_words(z):
+            for g in range(S // GATHER):
+                nc.vector.tensor_copy(
+                    x_codes[z][:, g * GATHER : (g + 1) * GATHER],
+                    word_window[z][:].bitcast(U32).indirect(offsets[:, g * GATHER // 16 : (g + 1) * GATHER // 16]),
+                )
+
+        h_bank = [ps.tile([P, PACK, CHUNK], F32, name="h_bank%d" % c) for c in range(CHUNKS)]
+        out_bank = [ps.tile([P, M_TILES, CHUNK], F32, name="out_bank%d" % c) for c in range(CHUNKS)]
+
+        def x_operand(z, c):
+            cols = slice(c * CHUNK, (c + 1) * CHUNK)
+            return x_codes[z][:, cols].bitcast(FP8X4), x_plane[:, z * S + c * CHUNK : z * S + (c + 1) * CHUNK]
+
+        def h_passes(z, c):
+            rhs, rhs_scale = x_operand(z, c)
+            for t in range(PACK):
+                nc.tensor.matmul_mx(
+                    out=h_bank[c][:, t, :],
+                    lhsT=w2_codes[z][:, t * P : (t + 1) * P].bitcast(FP8X4),
+                    lhsT_scale=w2_plane[z][:, t * P : (t + 1) * P],
+                    rhs=rhs,
+                    rhs_scale=rhs_scale,
+                    start=(z == 0 and t == 0),
+                    stop=(z == PASSES - 1 and t == PACK - 1),
+                )
+
+        def w1_passes(z, c):
+            rhs, rhs_scale = x_operand(z, c)
+            for m in range(M_TILES):
+                nc.tensor.matmul_mx(
+                    out=out_bank[c][:, m, :],
+                    lhsT=w1_codes[:, z, 2 * m * P : 2 * (m + 1) * P].bitcast(FP4X4),
+                    lhsT_scale=w1_plane[:, z, m * P : (m + 1) * P],
+                    rhs=rhs,
+                    rhs_scale=rhs_scale,
+                    start=(z == 0 and m == 0),
+                    stop=False,
+                )
+
+        gather_words(0)
+        for c in range(CHUNKS):
+            h_passes(0, c)
+            w1_passes(0, c)
+        gather_words(1)
+        for c in range(CHUNKS):
+            w1_passes(1, c)
+
+        for u in range(2):
+            grouped = sb.tile([P, PACK, HALF, PACK], BF16, name="grouped_last%d" % u, align_bytes=64)
+            deal(nc.scalar.copy, grouped, w2_last[u], 0, SCALAR_SHARE)
+            deal(nc.vector.tensor_copy, grouped, w2_last[u], SCALAR_SHARE, HALF)
+            for t in range(PACK):
+                cols = slice(t * P + u * HALF, t * P + (u + 1) * HALF)
+                nc.vector.quantize_mx(
+                    out=w2_codes[1][:, cols].bitcast(FP8X4),
+                    scales=w2_plane[1][:, cols],
+                    in_=grouped[:, t, :, :].rearrange("p m j -> p (m j)"),
+                )
+
+        for c in range(CHUNKS):
+            h_passes(1, c)
+
+        h_codes = [sb.tile([P, CHUNK], U32, name="h_codes%d" % c, align_bytes=64) for c in range(CHUNKS)]
+        h_plane = [sb.tile([P, CHUNK], U8, name="h_plane%d" % c, align_bytes=64) for c in range(CHUNKS)]
+        h_copy = [nc.scalar.copy, nc.vector.tensor_copy, nc.scalar.copy, nc.scalar.copy]
+        out_copy = [nc.scalar.copy, nc.scalar.copy, nc.vector.tensor_copy, nc.scalar.copy]
+        h_rounded = [sb.tile([P, CHUNK, PACK], BF16, name="h_rounded%d" % c, align_bytes=64) for c in range(CHUNKS)]
+        for c in range(CHUNKS):
+            h_copy[c](h_rounded[c][:], h_bank[c][:].rearrange("p t s -> p s t"))
+        out_rows = out.rearrange("(m p) s -> p m s", p=P)
+        for c in range(CHUNKS):
+            nc.vector.quantize_mx(
+                out=h_codes[c][:].bitcast(FP8X4),
+                scales=h_plane[c][:],
+                in_=h_rounded[c][:].rearrange("p s t -> p (s t)"),
+            )
+            for m in range(M_TILES):
+                nc.tensor.matmul_mx(
+                    out=out_bank[c][:, m, :],
+                    lhsT=w3_codes[:, 2 * m * P : 2 * (m + 1) * P].bitcast(FP4X4),
+                    lhsT_scale=w3_plane[:, m * P : (m + 1) * P],
+                    rhs=h_codes[c][:].bitcast(FP8X4),
+                    rhs_scale=h_plane[c][:],
+                    start=False,
+                    stop=(m == M_TILES - 1),
+                )
+        for c in range(CHUNKS):
+            result = sb.tile([P, M_TILES, CHUNK], F32, name="result%d" % c)
+            out_copy[c](result[:], out_bank[c][:])
+            nc.sync.dma_start(out_rows[:, :, c * CHUNK : (c + 1) * CHUNK], result[:])

@@ -23,7 +23,7 @@ CHUNKS = S // CHUNK
 GATHER = 256
 M_TILES = N // P
 HALF = P // 2
-SCALAR_SHARE = 24
+SCALAR_SHARE = 56
 
 
 def tile_picked_phlora_none_p_kernel(
@@ -32,14 +32,15 @@ def tile_picked_phlora_none_p_kernel(
     nc = tc.nc
     with ExitStack() as ctx:
         sb = ctx.enter_context(tc.tile_pool(name="sb", bufs=1))
+        shared = ctx.enter_context(tc.tile_pool(name="shared", bufs=1))
         ps = ctx.enter_context(tc.psum_pool(name="ps", bufs=1))
 
         offsets = sb.tile([P, S // 16], U16, name="offsets")
         nc.sync.dma_start(offsets[:], offs)
 
-        byte_window = sb.tile([P, T], U8, name="byte_window", align_bytes=64)
+        byte_window = shared.tile([P, T], U8, name="byte_window", offset=4 * T - 512, align_bytes=64)
         nc.gpsimd.memset(byte_window[:].bitcast(I32), 0)
-        nc.scalar.dma_start(
+        nc.sync.dma_start(
             byte_window[0:P:4, :].bitcast(I32), x_scales.rearrange("z q c -> q z c").bitcast(I32)
         )
         warm_in = sb.tile([P, 1], F32, name="warm_in")
@@ -49,62 +50,56 @@ def tile_picked_phlora_none_p_kernel(
         x_plane = sb.tile([P, PASSES * S], U8, name="x_plane", align_bytes=64)
         nc.vector.memset(x_plane[:].bitcast(I32), 0)
 
-        w1_codes = sb.tile([P, PASSES, 2 * N], U8, name="w1_codes", align_bytes=64)
-        nc.sync.dma_start(w1_codes[:].bitcast(I32), w1_words.rearrange("z p b -> p z b").bitcast(I32))
-        w3_codes = sb.tile([P, 2 * N], U8, name="w3_codes", align_bytes=64)
-        nc.sync.dma_start(w3_codes[:].bitcast(I32), w3_words[0].bitcast(I32))
-
-        w1_plane = sb.tile([P, PASSES, N], U8, name="w1_plane", align_bytes=64)
-        w3_plane = sb.tile([P, N], U8, name="w3_plane", align_bytes=64)
-        nc.vector.memset(w1_plane[:].bitcast(I32), 0)
-        nc.vector.memset(w3_plane[:].bitcast(I32), 0)
-        for q in range(4):
-            nc.gpsimd.dma_start(
-                w1_plane[32 * q : 32 * q + 4, :, :].bitcast(I32),
-                w1_scales[:, 4 * q : 4 * q + 4, :].rearrange("z r n -> r z n").bitcast(I32),
-            )
-        for q in range(4):
-            nc.gpsimd.dma_start(
-                w3_plane[32 * q : 32 * q + 4, :].bitcast(I32),
-                w3_scales[0, 4 * q : 4 * q + 4, :].bitcast(I32),
-            )
+        w_rows = sb.tile([P, N + P], U8, name="w_rows", align_bytes=64)
+        for z in range(PASSES):
+            nc.sync.dma_start(w_rows[4 * z : P : 8, 0:N].bitcast(I32), w1_scales[z].bitcast(I32))
+        nc.sync.dma_start(
+            w_rows[0:P:4, N : N + P].bitcast(I32), w3_scales[0].rearrange("q (m n) -> (q m) n", n=P).bitcast(I32)
+        )
 
         w2_first = sb.tile([P, PACK, H], F32, name="w2_first")
-        nc.sync.dma_start(w2_first[:], w2[0:K_PASS, :].rearrange("(p j) c -> p j c", j=PACK))
-        word_window = [sb.tile([P, T], I32, name="word_window%d" % z) for z in range(PASSES)]
-        for z in range(PASSES):
-            nc.sync.dma_start(word_window[z][:], x_words[z].rearrange("p c r -> p (c r)").bitcast(I32))
+        w2_first_rows = w2[0:K_PASS, :].rearrange("(p j) c -> p j c", j=PACK)
+        for j0 in (0, 2):
+            nc.sync.dma_start(w2_first[:, j0 : j0 + 2, :], w2_first_rows[:, j0 : j0 + 2, :])
+        word_window = [sb.tile([P, T], I32, name="word_window0")]
+        nc.sync.dma_start(word_window[0][:], x_words[0].rearrange("p c r -> p (c r)").bitcast(I32))
+        w2_last = sb.tile([P, PACK, H], F32, name="w2_last")
+        nc.sync.dma_start(w2_last[:], w2[K_PASS:K, :].rearrange("(p j) c -> p j c", j=PACK))
 
-        def load_w2_last(u, tag):
-            raw = sb.tile([P, PACK, H // 2], F32, name="w2_last%d" % u, tag=tag, align_bytes=64)
-            nc.sync.dma_start(
-                raw[:], w2[K_PASS:K, u * H // 2 : (u + 1) * H // 2].rearrange("(p j) c -> p j c", j=PACK)
-            )
-            return raw
-
-        w2_last = [load_w2_last(0, "w2_last0")]
-
-        picked_bytes = sb.tile([P, S], U8, name="picked_bytes", tag="after_moves", align_bytes=64)
+        picked_bytes = sb.tile([P, S], U8, name="picked_bytes", align_bytes=64)
         nc.vector.tensor_copy(picked_bytes[:], byte_window[:].indirect(offsets[:]))
         for q in range(4):
-            nc.scalar.dma_start(
+            nc.sync.dma_start(
                 x_plane[32 * q : 32 * q + 4, :].bitcast(I32).rearrange("p (z s) -> p z s", z=PASSES),
                 picked_bytes[32 * q : 32 * q + 32 : 4, :].bitcast(I32),
             )
 
-        w2_last.append(load_w2_last(1, "after_moves"))
+        word_window.append(shared.tile([P, T], I32, name="word_window1", offset=0, align_bytes=64))
+        nc.sync.dma_start(word_window[1][:], x_words[1].rearrange("p c r -> p (c r)").bitcast(I32))
+        w1_codes = shared.tile([P, PASSES, 2 * N], U8, name="w1_codes", offset=4 * T + 1280, align_bytes=64)
+        nc.sync.dma_start(w1_codes[:].bitcast(I32), w1_words.rearrange("z p b -> p z b").bitcast(I32))
+        w_plane = shared.tile([P, 2, N + P], U8, name="w_plane", offset=4 * T, align_bytes=64)
+        nc.vector.memset(w_plane[:].bitcast(I32), 0)
+        for q in range(4):
+            nc.sync.dma_start(
+                w_plane[32 * q : 32 * q + 4, :, :].bitcast(I32),
+                w_rows[32 * q : 32 * q + 32 : 4, :].bitcast(I32),
+            )
+        w3_codes = shared.tile([P, 2 * N], U8, name="w3_codes", offset=4 * T + 768, align_bytes=64)
+        nc.sync.dma_start(w3_codes[:].bitcast(I32), w3_words[0].bitcast(I32))
 
         w2_codes = [sb.tile([P, H], U32, name="w2_codes%d" % z, align_bytes=64) for z in range(PASSES)]
         w2_plane = [sb.tile([P, H], U8, name="w2_plane%d" % z, align_bytes=64) for z in range(PASSES)]
 
-        def deal(copy, grouped, raw, m0, m1):
+        def deal(copy, grouped, raw, m0, m1, j0=0, j1=PACK):
             copy(
-                grouped[:, :, m0:m1, :].rearrange("p t m j -> p m j t"),
-                raw[:].rearrange("p j (m t) -> p m j t", t=PACK)[:, m0:m1, :, :],
+                grouped[:, :, m0:m1, j0:j1].rearrange("p t m j -> p m j t"),
+                raw.rearrange("p j (m t) -> p m j t", t=PACK)[:, m0:m1, :, :],
             )
 
         grouped_first = sb.tile([P, PACK, P, PACK], BF16, name="grouped_first", align_bytes=64)
-        deal(nc.scalar.copy, grouped_first, w2_first, 0, P)
+        deal(nc.scalar.copy, grouped_first, w2_first[:], 0, SCALAR_SHARE)
+        deal(nc.vector.tensor_copy, grouped_first, w2_first[:], SCALAR_SHARE, P)
         nc.vector.quantize_mx(
             out=w2_codes[0][:].bitcast(FP8X4),
             scales=w2_plane[0][:],
@@ -146,7 +141,7 @@ def tile_picked_phlora_none_p_kernel(
                 nc.tensor.matmul_mx(
                     out=out_bank[c][:, m, :],
                     lhsT=w1_codes[:, z, 2 * m * P : 2 * (m + 1) * P].bitcast(FP4X4),
-                    lhsT_scale=w1_plane[:, z, m * P : (m + 1) * P],
+                    lhsT_scale=w_plane[:, z, m * P : (m + 1) * P],
                     rhs=rhs,
                     rhs_scale=rhs_scale,
                     start=(z == 0 and m == 0),
@@ -156,30 +151,26 @@ def tile_picked_phlora_none_p_kernel(
         gather_words(0)
         for c in range(CHUNKS):
             h_passes(0, c)
-            w1_passes(0, c)
+        grouped_last = sb.tile([P, PACK, P, PACK], BF16, name="grouped_last", align_bytes=64)
+        deal(nc.scalar.copy, grouped_last, w2_last[:], 0, SCALAR_SHARE)
+        deal(nc.vector.tensor_copy, grouped_last, w2_last[:], SCALAR_SHARE, P)
+        nc.vector.quantize_mx(
+            out=w2_codes[1][:].bitcast(FP8X4),
+            scales=w2_plane[1][:],
+            in_=grouped_last[:].rearrange("p t m j -> p (t m j)"),
+        )
+
         gather_words(1)
         for c in range(CHUNKS):
-            w1_passes(1, c)
-
-        for u in range(2):
-            grouped = sb.tile([P, PACK, HALF, PACK], BF16, name="grouped_last%d" % u, align_bytes=64)
-            deal(nc.scalar.copy, grouped, w2_last[u], 0, SCALAR_SHARE)
-            deal(nc.vector.tensor_copy, grouped, w2_last[u], SCALAR_SHARE, HALF)
-            for t in range(PACK):
-                cols = slice(t * P + u * HALF, t * P + (u + 1) * HALF)
-                nc.vector.quantize_mx(
-                    out=w2_codes[1][:, cols].bitcast(FP8X4),
-                    scales=w2_plane[1][:, cols],
-                    in_=grouped[:, t, :, :].rearrange("p m j -> p (m j)"),
-                )
-
-        for c in range(CHUNKS):
             h_passes(1, c)
+        for c in range(CHUNKS):
+            for z in range(PASSES):
+                w1_passes(z, c)
 
         h_codes = [sb.tile([P, CHUNK], U32, name="h_codes%d" % c, align_bytes=64) for c in range(CHUNKS)]
         h_plane = [sb.tile([P, CHUNK], U8, name="h_plane%d" % c, align_bytes=64) for c in range(CHUNKS)]
         h_copy = [nc.scalar.copy, nc.vector.tensor_copy, nc.scalar.copy, nc.scalar.copy]
-        out_copy = [nc.scalar.copy, nc.scalar.copy, nc.vector.tensor_copy, nc.scalar.copy]
+        out_copy = [nc.scalar.copy, nc.vector.tensor_copy, nc.scalar.copy, nc.vector.tensor_copy]
         h_rounded = [sb.tile([P, CHUNK, PACK], BF16, name="h_rounded%d" % c, align_bytes=64) for c in range(CHUNKS)]
         for c in range(CHUNKS):
             h_copy[c](h_rounded[c][:], h_bank[c][:].rearrange("p t s -> p s t"))
@@ -194,7 +185,7 @@ def tile_picked_phlora_none_p_kernel(
                 nc.tensor.matmul_mx(
                     out=out_bank[c][:, m, :],
                     lhsT=w3_codes[:, 2 * m * P : 2 * (m + 1) * P].bitcast(FP4X4),
-                    lhsT_scale=w3_plane[:, m * P : (m + 1) * P],
+                    lhsT_scale=w_plane[:, m, N : N + P],
                     rhs=h_codes[c][:].bitcast(FP8X4),
                     rhs_scale=h_plane[c][:],
                     start=False,

@@ -59,8 +59,8 @@ def tile_picked_phlora_none_p_kernel(
 
         w2_first = sb.tile([P, PACK, H], F32, name="w2_first")
         w2_first_rows = w2[0:K_PASS, :].rearrange("(p j) c -> p j c", j=PACK)
-        for j0 in (0, 2):
-            nc.sync.dma_start(w2_first[:, j0 : j0 + 2, :], w2_first_rows[:, j0 : j0 + 2, :])
+        nc.scalar.dma_start(w2_first[:, 0:2, :], w2_first_rows[:, 0:2, :])
+        nc.sync.dma_start(w2_first[:, 2:4, :], w2_first_rows[:, 2:4, :])
         word_window = [sb.tile([P, T], I32, name="word_window0")]
         nc.sync.dma_start(word_window[0][:], x_words[0].rearrange("p c r -> p (c r)").bitcast(I32))
         w2_last = sb.tile([P, PACK, H], F32, name="w2_last")
@@ -106,12 +106,15 @@ def tile_picked_phlora_none_p_kernel(
             in_=grouped_first[:].rearrange("p t m j -> p (t m j)"),
         )
 
-        x_codes = [sb.tile([P, S], U32, name="x_codes%d" % z, align_bytes=64) for z in range(PASSES)]
+        x_codes = [
+            [sb.tile([P, GATHER], U32, name="x_codes%d_%d" % (z, g), align_bytes=64) for g in range(S // GATHER)]
+            for z in range(PASSES)
+        ]
 
         def gather_words(z):
             for g in range(S // GATHER):
                 nc.vector.tensor_copy(
-                    x_codes[z][:, g * GATHER : (g + 1) * GATHER],
+                    x_codes[z][g][:],
                     word_window[z][:].bitcast(U32).indirect(offsets[:, g * GATHER // 16 : (g + 1) * GATHER // 16]),
                 )
 
@@ -119,8 +122,8 @@ def tile_picked_phlora_none_p_kernel(
         out_bank = [ps.tile([P, M_TILES, CHUNK], F32, name="out_bank%d" % c) for c in range(CHUNKS)]
 
         def x_operand(z, c):
-            cols = slice(c * CHUNK, (c + 1) * CHUNK)
-            return x_codes[z][:, cols].bitcast(FP8X4), x_plane[:, z * S + c * CHUNK : z * S + (c + 1) * CHUNK]
+            g, first = divmod(c * CHUNK, GATHER)
+            return x_codes[z][g][:, first : first + CHUNK].bitcast(FP8X4), x_plane[:, z * S + c * CHUNK : z * S + (c + 1) * CHUNK]
 
         def h_passes(z, c):
             rhs, rhs_scale = x_operand(z, c)
@@ -144,7 +147,7 @@ def tile_picked_phlora_none_p_kernel(
                     lhsT_scale=w_plane[:, z, m * P : (m + 1) * P],
                     rhs=rhs,
                     rhs_scale=rhs_scale,
-                    start=(z == 0 and m == 0),
+                    start=(z == PASSES - 1 and m == 0),
                     stop=False,
                 )
 
@@ -164,13 +167,13 @@ def tile_picked_phlora_none_p_kernel(
         for c in range(CHUNKS):
             h_passes(1, c)
         for c in range(CHUNKS):
-            for z in range(PASSES):
+            for z in reversed(range(PASSES)):
                 w1_passes(z, c)
 
         h_codes = [sb.tile([P, CHUNK], U32, name="h_codes%d" % c, align_bytes=64) for c in range(CHUNKS)]
         h_plane = [sb.tile([P, CHUNK], U8, name="h_plane%d" % c, align_bytes=64) for c in range(CHUNKS)]
         h_copy = [nc.scalar.copy, nc.vector.tensor_copy, nc.scalar.copy, nc.scalar.copy]
-        out_copy = [nc.scalar.copy, nc.vector.tensor_copy, nc.scalar.copy, nc.vector.tensor_copy]
+        out_copy = [nc.scalar.copy, nc.scalar.copy, nc.scalar.copy, nc.vector.tensor_copy]
         h_rounded = [sb.tile([P, CHUNK, PACK], BF16, name="h_rounded%d" % c, align_bytes=64) for c in range(CHUNKS)]
         for c in range(CHUNKS):
             h_copy[c](h_rounded[c][:], h_bank[c][:].rearrange("p t s -> p s t"))

@@ -24,6 +24,7 @@ GATHER = 256
 M_TILES = N // P
 HALF = P // 2
 SCALAR_SHARE = 56
+WARM_PASSES = 6
 
 
 def tile_picked_phlora_none_p_kernel(
@@ -152,6 +153,16 @@ def tile_picked_phlora_none_p_kernel(
                 )
 
         gather_words(0)
+        for i in range(WARM_PASSES):
+            nc.tensor.matmul_mx(
+                out=out_bank[i % CHUNKS][:].rearrange("p m s -> p (m s)"),
+                lhsT=w2_codes[0][:, 0:P].bitcast(FP8X4),
+                lhsT_scale=w2_plane[0][:, 0:P],
+                rhs=x_codes[0][0][:].bitcast(FP8X4),
+                rhs_scale=w2_plane[0][:, 0:GATHER],
+                start=True,
+                stop=True,
+            )
         for c in range(CHUNKS):
             h_passes(0, c)
         grouped_last = sb.tile([P, PACK, P, PACK], BF16, name="grouped_last", align_bytes=64)

@@ -23,8 +23,9 @@ CHUNKS = S // CHUNK
 GATHER = 256
 M_TILES = N // P
 HALF = P // 2
-SCALAR_SHARE = 56
-WARM_PASSES = 6
+SCALAR_SHARE = 48
+QUADRANTS = (0, 2, 1, 3)
+EARLY_CHUNKS = 2
 
 
 def tile_picked_phlora_none_p_kernel(
@@ -36,32 +37,25 @@ def tile_picked_phlora_none_p_kernel(
         shared = ctx.enter_context(tc.tile_pool(name="shared", bufs=1))
         ps = ctx.enter_context(tc.psum_pool(name="ps", bufs=1))
 
+        w2_first = sb.tile([P, PACK, H], F32, name="w2_first")
+        nc.sync.dma_start(w2_first[:], w2[0:K_PASS, :].rearrange("(p j) c -> p j c", j=PACK))
         offsets = sb.tile([P, S // 16], U16, name="offsets")
         nc.sync.dma_start(offsets[:], offs)
 
-        byte_window = shared.tile([P, T], U8, name="byte_window", offset=4 * T - 512, align_bytes=64)
-        nc.gpsimd.memset(byte_window[:].bitcast(I32), 0)
+        byte_window = shared.tile([P, T], U8, name="byte_window", offset=4 * T - 64, align_bytes=64)
+        nc.vector.memset(byte_window[:].bitcast(I32), 0)
         nc.sync.dma_start(
             byte_window[0:P:4, :].bitcast(I32), x_scales.rearrange("z q c -> q z c").bitcast(I32)
         )
-        warm_in = sb.tile([P, 1], F32, name="warm_in")
-        warm_out = sb.tile([P, 1], F32, name="warm_out")
-        nc.gpsimd.memset(warm_in[:], 0.0)
-        nc.scalar.copy(warm_out[:], warm_in[:])
         x_plane = sb.tile([P, PASSES * S], U8, name="x_plane", align_bytes=64)
         nc.vector.memset(x_plane[:].bitcast(I32), 0)
 
         w_rows = sb.tile([P, N + P], U8, name="w_rows", align_bytes=64)
-        for z in range(PASSES):
-            nc.sync.dma_start(w_rows[4 * z : P : 8, 0:N].bitcast(I32), w1_scales[z].bitcast(I32))
+        nc.sync.dma_start(w_rows[0:P:4, 0:N].bitcast(I32), w1_scales.rearrange("z q n -> q z n").bitcast(I32))
         nc.sync.dma_start(
             w_rows[0:P:4, N : N + P].bitcast(I32), w3_scales[0].rearrange("q (m n) -> (q m) n", n=P).bitcast(I32)
         )
 
-        w2_first = sb.tile([P, PACK, H], F32, name="w2_first")
-        w2_first_rows = w2[0:K_PASS, :].rearrange("(p j) c -> p j c", j=PACK)
-        nc.scalar.dma_start(w2_first[:, 0:2, :], w2_first_rows[:, 0:2, :])
-        nc.sync.dma_start(w2_first[:, 2:4, :], w2_first_rows[:, 2:4, :])
         word_window = [sb.tile([P, T], I32, name="word_window0")]
         nc.sync.dma_start(word_window[0][:], x_words[0].rearrange("p c r -> p (c r)").bitcast(I32))
         w2_last = sb.tile([P, PACK, H], F32, name="w2_last")
@@ -69,7 +63,7 @@ def tile_picked_phlora_none_p_kernel(
 
         picked_bytes = sb.tile([P, S], U8, name="picked_bytes", align_bytes=64)
         nc.vector.tensor_copy(picked_bytes[:], byte_window[:].indirect(offsets[:]))
-        for q in range(4):
+        for q in QUADRANTS:
             nc.sync.dma_start(
                 x_plane[32 * q : 32 * q + 4, :].bitcast(I32).rearrange("p (z s) -> p z s", z=PASSES),
                 picked_bytes[32 * q : 32 * q + 32 : 4, :].bitcast(I32),
@@ -77,16 +71,20 @@ def tile_picked_phlora_none_p_kernel(
 
         word_window.append(shared.tile([P, T], I32, name="word_window1", offset=0, align_bytes=64))
         nc.sync.dma_start(word_window[1][:], x_words[1].rearrange("p c r -> p (c r)").bitcast(I32))
-        w1_codes = shared.tile([P, PASSES, 2 * N], U8, name="w1_codes", offset=4 * T + 1280, align_bytes=64)
-        nc.sync.dma_start(w1_codes[:].bitcast(I32), w1_words.rearrange("z p b -> p z b").bitcast(I32))
         w_plane = shared.tile([P, 2, N + P], U8, name="w_plane", offset=4 * T, align_bytes=64)
         nc.vector.memset(w_plane[:].bitcast(I32), 0)
-        for q in range(4):
+        w1_codes = [
+            shared.tile([P, 2 * N], U8, name="w1_codes%d" % z, offset=4 * T + 768 + 512 * z, align_bytes=64)
+            for z in range(PASSES)
+        ]
+        nc.sync.dma_start(w1_codes[0][:].bitcast(I32), w1_words[0].bitcast(I32))
+        for q in QUADRANTS:
             nc.sync.dma_start(
                 w_plane[32 * q : 32 * q + 4, :, :].bitcast(I32),
                 w_rows[32 * q : 32 * q + 32 : 4, :].bitcast(I32),
             )
-        w3_codes = shared.tile([P, 2 * N], U8, name="w3_codes", offset=4 * T + 768, align_bytes=64)
+        nc.sync.dma_start(w1_codes[1][:].bitcast(I32), w1_words[1].bitcast(I32))
+        w3_codes = shared.tile([P, 2 * N], U8, name="w3_codes", offset=4 * T + 1792, align_bytes=64)
         nc.sync.dma_start(w3_codes[:].bitcast(I32), w3_words[0].bitcast(I32))
 
         w2_codes = [sb.tile([P, H], U32, name="w2_codes%d" % z, align_bytes=64) for z in range(PASSES)]
@@ -139,30 +137,20 @@ def tile_picked_phlora_none_p_kernel(
                     stop=(z == PASSES - 1 and t == PACK - 1),
                 )
 
-        def w1_passes(z, c):
+        def w1_passes(z, c, first):
             rhs, rhs_scale = x_operand(z, c)
             for m in range(M_TILES):
                 nc.tensor.matmul_mx(
                     out=out_bank[c][:, m, :],
-                    lhsT=w1_codes[:, z, 2 * m * P : 2 * (m + 1) * P].bitcast(FP4X4),
+                    lhsT=w1_codes[z][:, 2 * m * P : 2 * (m + 1) * P].bitcast(FP4X4),
                     lhsT_scale=w_plane[:, z, m * P : (m + 1) * P],
                     rhs=rhs,
                     rhs_scale=rhs_scale,
-                    start=(z == PASSES - 1 and m == 0),
+                    start=(first and m == 0),
                     stop=False,
                 )
 
         gather_words(0)
-        for i in range(WARM_PASSES):
-            nc.tensor.matmul_mx(
-                out=out_bank[i % CHUNKS][:].rearrange("p m s -> p (m s)"),
-                lhsT=w2_codes[0][:, 0:P].bitcast(FP8X4),
-                lhsT_scale=w2_plane[0][:, 0:P],
-                rhs=x_codes[0][0][:].bitcast(FP8X4),
-                rhs_scale=w2_plane[0][:, 0:GATHER],
-                start=True,
-                stop=True,
-            )
         for c in range(CHUNKS):
             h_passes(0, c)
         grouped_last = sb.tile([P, PACK, P, PACK], BF16, name="grouped_last", align_bytes=64)
@@ -177,19 +165,19 @@ def tile_picked_phlora_none_p_kernel(
         gather_words(1)
         for c in range(CHUNKS):
             h_passes(1, c)
-        for c in range(CHUNKS):
-            for z in reversed(range(PASSES)):
-                w1_passes(z, c)
 
         h_codes = [sb.tile([P, CHUNK], U32, name="h_codes%d" % c, align_bytes=64) for c in range(CHUNKS)]
         h_plane = [sb.tile([P, CHUNK], U8, name="h_plane%d" % c, align_bytes=64) for c in range(CHUNKS)]
-        h_copy = [nc.scalar.copy, nc.vector.tensor_copy, nc.scalar.copy, nc.scalar.copy]
-        out_copy = [nc.scalar.copy, nc.scalar.copy, nc.scalar.copy, nc.vector.tensor_copy]
+        h_copy = [nc.vector.tensor_copy, nc.scalar.copy, nc.vector.tensor_copy, nc.scalar.copy]
+        out_copy = [nc.scalar.copy, nc.vector.tensor_copy, nc.scalar.copy, nc.vector.tensor_copy]
         h_rounded = [sb.tile([P, CHUNK, PACK], BF16, name="h_rounded%d" % c, align_bytes=64) for c in range(CHUNKS)]
         for c in range(CHUNKS):
             h_copy[c](h_rounded[c][:], h_bank[c][:].rearrange("p t s -> p s t"))
         out_rows = out.rearrange("(m p) s -> p m s", p=P)
         for c in range(CHUNKS):
+            order = range(PASSES) if c < EARLY_CHUNKS else reversed(range(PASSES))
+            for i, z in enumerate(order):
+                w1_passes(z, c, i == 0)
             nc.vector.quantize_mx(
                 out=h_codes[c][:].bitcast(FP8X4),
                 scales=h_plane[c][:],

@@ -23,7 +23,7 @@ CHUNKS = S // CHUNK
 GATHER = 256
 M_TILES = N // P
 HALF = P // 2
-SCALAR_SHARE = 48
+SCALAR_SHARE = (64, 56)
 QUADRANTS = (0, 2, 1, 3)
 EARLY_CHUNKS = 2
 
@@ -37,8 +37,6 @@ def tile_picked_phlora_none_p_kernel(
         shared = ctx.enter_context(tc.tile_pool(name="shared", bufs=1))
         ps = ctx.enter_context(tc.psum_pool(name="ps", bufs=1))
 
-        w2_first = sb.tile([P, PACK, H], F32, name="w2_first")
-        nc.sync.dma_start(w2_first[:], w2[0:K_PASS, :].rearrange("(p j) c -> p j c", j=PACK))
         offsets = sb.tile([P, S // 16], U16, name="offsets")
         nc.sync.dma_start(offsets[:], offs)
 
@@ -56,6 +54,10 @@ def tile_picked_phlora_none_p_kernel(
             w_rows[0:P:4, N : N + P].bitcast(I32), w3_scales[0].rearrange("q (m n) -> (q m) n", n=P).bitcast(I32)
         )
 
+        w2_first = sb.tile([P, PACK, H], F32, name="w2_first")
+        w2_first_rows = w2[0:K_PASS, :].rearrange("(p j) c -> p j c", j=PACK)
+        nc.scalar.dma_start(w2_first[:, 0:2, :], w2_first_rows[:, 0:2, :])
+        nc.sync.dma_start(w2_first[:, 2:4, :], w2_first_rows[:, 2:4, :])
         word_window = [sb.tile([P, T], I32, name="word_window0")]
         nc.sync.dma_start(word_window[0][:], x_words[0].rearrange("p c r -> p (c r)").bitcast(I32))
         w2_last = sb.tile([P, PACK, H], F32, name="w2_last")
@@ -93,12 +95,13 @@ def tile_picked_phlora_none_p_kernel(
         def deal(copy, grouped, raw, m0, m1, j0=0, j1=PACK):
             copy(
                 grouped[:, :, m0:m1, j0:j1].rearrange("p t m j -> p m j t"),
-                raw.rearrange("p j (m t) -> p m j t", t=PACK)[:, m0:m1, :, :],
+                raw.rearrange("p j (m t) -> p m j t", t=PACK)[:, m0:m1, j0:j1, :],
             )
 
         grouped_first = sb.tile([P, PACK, P, PACK], BF16, name="grouped_first", align_bytes=64)
-        deal(nc.scalar.copy, grouped_first, w2_first[:], 0, SCALAR_SHARE)
-        deal(nc.vector.tensor_copy, grouped_first, w2_first[:], SCALAR_SHARE, P)
+        for j0 in (0, 2):
+            deal(nc.scalar.copy, grouped_first, w2_first[:], 0, SCALAR_SHARE[0], j0, j0 + 2)
+        deal(nc.vector.tensor_copy, grouped_first, w2_first[:], SCALAR_SHARE[0], P)
         nc.vector.quantize_mx(
             out=w2_codes[0][:].bitcast(FP8X4),
             scales=w2_plane[0][:],
@@ -154,8 +157,8 @@ def tile_picked_phlora_none_p_kernel(
         for c in range(CHUNKS):
             h_passes(0, c)
         grouped_last = sb.tile([P, PACK, P, PACK], BF16, name="grouped_last", align_bytes=64)
-        deal(nc.scalar.copy, grouped_last, w2_last[:], 0, SCALAR_SHARE)
-        deal(nc.vector.tensor_copy, grouped_last, w2_last[:], SCALAR_SHARE, P)
+        deal(nc.scalar.copy, grouped_last, w2_last[:], 0, SCALAR_SHARE[1])
+        deal(nc.vector.tensor_copy, grouped_last, w2_last[:], SCALAR_SHARE[1], P)
         nc.vector.quantize_mx(
             out=w2_codes[1][:].bitcast(FP8X4),
             scales=w2_plane[1][:],

@@ -23,7 +23,7 @@ CHUNKS = S // CHUNK
 GATHER = 256
 M_TILES = N // P
 HALF = P // 2
-SCALAR_SHARE = (64, 56)
+SCALAR_SHARE = (64, 44)
 QUADRANTS = (0, 2, 1, 3)
 EARLY_CHUNKS = 2
 

@@ -35,6 +35,7 @@ def tile_picked_phlora_none_p_kernel(
     with ExitStack() as ctx:
         sb = ctx.enter_context(tc.tile_pool(name="sb", bufs=1))
         shared = ctx.enter_context(tc.tile_pool(name="shared", bufs=1))
+        early = ctx.enter_context(tc.tile_pool(name="early", bufs=1))
         ps = ctx.enter_context(tc.psum_pool(name="ps", bufs=1))
 
         offsets = sb.tile([P, S // 16], U16, name="offsets")
@@ -54,14 +55,14 @@ def tile_picked_phlora_none_p_kernel(
             w_rows[0:P:4, N : N + P].bitcast(I32), w3_scales[0].rearrange("q (m n) -> (q m) n", n=P).bitcast(I32)
         )
 
-        w2_first = sb.tile([P, PACK, H], F32, name="w2_first")
+        w2_first = early.tile([P, PACK, H], F32, name="w2_first", offset=0, align_bytes=64)
         w2_first_rows = w2[0:K_PASS, :].rearrange("(p j) c -> p j c", j=PACK)
-        nc.scalar.dma_start(w2_first[:, 0:2, :], w2_first_rows[:, 0:2, :])
-        nc.sync.dma_start(w2_first[:, 2:4, :], w2_first_rows[:, 2:4, :])
+        nc.scalar.dma_start(w2_first[:], w2_first_rows)
         word_window = [sb.tile([P, T], I32, name="word_window0")]
         nc.sync.dma_start(word_window[0][:], x_words[0].rearrange("p c r -> p (c r)").bitcast(I32))
-        w2_last = sb.tile([P, PACK, H], F32, name="w2_last")
-        nc.sync.dma_start(w2_last[:], w2[K_PASS:K, :].rearrange("(p j) c -> p j c", j=PACK))
+        w2_last_rows = w2[K_PASS:K, :].rearrange("(p j) c -> p j c", j=PACK)
+        w2_last = [sb.tile([P, 3, H], F32, name="w2_last0")]
+        nc.sync.dma_start(w2_last[0][:], w2_last_rows[:, 0:3, :])
 
         picked_bytes = sb.tile([P, S], U8, name="picked_bytes", align_bytes=64)
         nc.vector.tensor_copy(picked_bytes[:], byte_window[:].indirect(offsets[:]))
@@ -71,6 +72,8 @@ def tile_picked_phlora_none_p_kernel(
                 picked_bytes[32 * q : 32 * q + 32 : 4, :].bitcast(I32),
             )
 
+        w2_last.append(shared.tile([P, 1, H], F32, name="w2_last1", offset=4 * T + 1920, align_bytes=64))
+        nc.sync.dma_start(w2_last[1][:], w2_last_rows[:, 3:4, :])
         word_window.append(shared.tile([P, T], I32, name="word_window1", offset=0, align_bytes=64))
         nc.sync.dma_start(word_window[1][:], x_words[1].rearrange("p c r -> p (c r)").bitcast(I32))
         w_plane = shared.tile([P, 2, N + P], U8, name="w_plane", offset=4 * T, align_bytes=64)
@@ -86,8 +89,6 @@ def tile_picked_phlora_none_p_kernel(
                 w_rows[32 * q : 32 * q + 32 : 4, :].bitcast(I32),
             )
         nc.sync.dma_start(w1_codes[1][:].bitcast(I32), w1_words[1].bitcast(I32))
-        w3_codes = shared.tile([P, 2 * N], U8, name="w3_codes", offset=4 * T + 1792, align_bytes=64)
-        nc.sync.dma_start(w3_codes[:].bitcast(I32), w3_words[0].bitcast(I32))
 
         w2_codes = [sb.tile([P, H], U32, name="w2_codes%d" % z, align_bytes=64) for z in range(PASSES)]
         w2_plane = [sb.tile([P, H], U8, name="w2_plane%d" % z, align_bytes=64) for z in range(PASSES)]
@@ -99,14 +100,16 @@ def tile_picked_phlora_none_p_kernel(
             )
 
         grouped_first = sb.tile([P, PACK, P, PACK], BF16, name="grouped_first", align_bytes=64)
-        for j0 in (0, 2):
-            deal(nc.scalar.copy, grouped_first, w2_first[:], 0, SCALAR_SHARE[0], j0, j0 + 2)
+        deal(nc.scalar.copy, grouped_first, w2_first[:], 0, SCALAR_SHARE[0])
         deal(nc.vector.tensor_copy, grouped_first, w2_first[:], SCALAR_SHARE[0], P)
         nc.vector.quantize_mx(
             out=w2_codes[0][:].bitcast(FP8X4),
             scales=w2_plane[0][:],
             in_=grouped_first[:].rearrange("p t m j -> p (t m j)"),
         )
+
+        w3_codes = early.tile([P, 2 * N], U8, name="w3_codes", offset=0, align_bytes=64)
+        nc.sync.dma_start(w3_codes[:].bitcast(I32), w3_words[0].bitcast(I32))
 
         x_codes = [
             [sb.tile([P, GATHER], U32, name="x_codes%d_%d" % (z, g), align_bytes=64) for g in range(S // GATHER)]
@@ -157,8 +160,12 @@ def tile_picked_phlora_none_p_kernel(
         for c in range(CHUNKS):
             h_passes(0, c)
         grouped_last = sb.tile([P, PACK, P, PACK], BF16, name="grouped_last", align_bytes=64)
-        deal(nc.scalar.copy, grouped_last, w2_last[:], 0, SCALAR_SHARE[1])
-        deal(nc.vector.tensor_copy, grouped_last, w2_last[:], SCALAR_SHARE[1], P)
+        for u, (j0, j1) in enumerate(((0, 3), (3, PACK))):
+            for copy, m0, m1 in ((nc.scalar.copy, 0, SCALAR_SHARE[1]), (nc.vector.tensor_copy, SCALAR_SHARE[1], P)):
+                copy(
+                    grouped_last[:, :, m0:m1, j0:j1].rearrange("p t m j -> p m j t"),
+                    w2_last[u][:].rearrange("p j (m t) -> p m j t", t=PACK)[:, m0:m1, :, :],
+                )
         nc.vector.quantize_mx(
             out=w2_codes[1][:].bitcast(FP8X4),
             scales=w2_plane[1][:],

@@ -25,7 +25,6 @@ M_TILES = N // P
 HALF = P // 2
 SCALAR_SHARE = (64, 44)
 QUADRANTS = (0, 2, 1, 3)
-EARLY_CHUNKS = 2
 
 
 def tile_picked_phlora_none_p_kernel(
@@ -78,17 +77,8 @@ def tile_picked_phlora_none_p_kernel(
         nc.sync.dma_start(word_window[1][:], x_words[1].rearrange("p c r -> p (c r)").bitcast(I32))
         w_plane = shared.tile([P, 2, N + P], U8, name="w_plane", offset=4 * T, align_bytes=64)
         nc.vector.memset(w_plane[:].bitcast(I32), 0)
-        w1_codes = [
-            shared.tile([P, 2 * N], U8, name="w1_codes%d" % z, offset=4 * T + 768 + 512 * z, align_bytes=64)
-            for z in range(PASSES)
-        ]
-        nc.sync.dma_start(w1_codes[0][:].bitcast(I32), w1_words[0].bitcast(I32))
-        for q in QUADRANTS:
-            nc.sync.dma_start(
-                w_plane[32 * q : 32 * q + 4, :, :].bitcast(I32),
-                w_rows[32 * q : 32 * q + 32 : 4, :].bitcast(I32),
-            )
-        nc.sync.dma_start(w1_codes[1][:].bitcast(I32), w1_words[1].bitcast(I32))
+        w1_codes = shared.tile([P, PASSES, 2 * N], U8, name="w1_codes", offset=4 * T + 768, align_bytes=64)
+        nc.sync.dma_start(w1_codes[:].bitcast(I32), w1_words.rearrange("z p n -> p z n").bitcast(I32))
 
         w2_codes = [sb.tile([P, H], U32, name="w2_codes%d" % z, align_bytes=64) for z in range(PASSES)]
         w2_plane = [sb.tile([P, H], U8, name="w2_plane%d" % z, align_bytes=64) for z in range(PASSES)]
@@ -110,6 +100,11 @@ def tile_picked_phlora_none_p_kernel(
 
         w3_codes = early.tile([P, 2 * N], U8, name="w3_codes", offset=0, align_bytes=64)
         nc.sync.dma_start(w3_codes[:].bitcast(I32), w3_words[0].bitcast(I32))
+        for q in QUADRANTS:
+            nc.sync.dma_start(
+                w_plane[32 * q : 32 * q + 4, :, :].bitcast(I32),
+                w_rows[32 * q : 32 * q + 32 : 4, :].bitcast(I32),
+            )
 
         x_codes = [
             [sb.tile([P, GATHER], U32, name="x_codes%d_%d" % (z, g), align_bytes=64) for g in range(S // GATHER)]
@@ -124,7 +119,8 @@ def tile_picked_phlora_none_p_kernel(
                 )
 
         h_bank = [ps.tile([P, PACK, CHUNK], F32, name="h_bank%d" % c) for c in range(CHUNKS)]
-        out_bank = [ps.tile([P, M_TILES, CHUNK], F32, name="out_bank%d" % c) for c in range(CHUNKS)]
+        out_bank = [ps.tile([P, M_TILES, CHUNK], F32, name="out_bank%d" % c) for c in range(CHUNKS - 1)]
+        out_part = [[out_bank[c][:, m, :] for m in range(M_TILES)] for c in range(CHUNKS - 1)]
 
         def x_operand(z, c):
             g, first = divmod(c * CHUNK, GATHER)
@@ -143,16 +139,16 @@ def tile_picked_phlora_none_p_kernel(
                     stop=(z == PASSES - 1 and t == PACK - 1),
                 )
 
-        def w1_passes(z, c, first):
+        def w1_passes(c, z):
             rhs, rhs_scale = x_operand(z, c)
             for m in range(M_TILES):
                 nc.tensor.matmul_mx(
-                    out=out_bank[c][:, m, :],
-                    lhsT=w1_codes[z][:, 2 * m * P : 2 * (m + 1) * P].bitcast(FP4X4),
+                    out=out_part[c][m],
+                    lhsT=w1_codes[:, z, 2 * m * P : 2 * (m + 1) * P].bitcast(FP4X4),
                     lhsT_scale=w_plane[:, z, m * P : (m + 1) * P],
                     rhs=rhs,
                     rhs_scale=rhs_scale,
-                    start=(first and m == 0),
+                    start=(z == 0 and (m == 0 or c == CHUNKS - 1)),
                     stop=False,
                 )
 
@@ -178,16 +174,15 @@ def tile_picked_phlora_none_p_kernel(
 
         h_codes = [sb.tile([P, CHUNK], U32, name="h_codes%d" % c, align_bytes=64) for c in range(CHUNKS)]
         h_plane = [sb.tile([P, CHUNK], U8, name="h_plane%d" % c, align_bytes=64) for c in range(CHUNKS)]
-        h_copy = [nc.vector.tensor_copy, nc.scalar.copy, nc.vector.tensor_copy, nc.scalar.copy]
-        out_copy = [nc.scalar.copy, nc.vector.tensor_copy, nc.scalar.copy, nc.vector.tensor_copy]
         h_rounded = [sb.tile([P, CHUNK, PACK], BF16, name="h_rounded%d" % c, align_bytes=64) for c in range(CHUNKS)]
-        for c in range(CHUNKS):
-            h_copy[c](h_rounded[c][:], h_bank[c][:].rearrange("p t s -> p s t"))
         out_rows = out.rearrange("(m p) s -> p m s", p=P)
+        copies = (nc.vector.tensor_copy, nc.scalar.copy)
         for c in range(CHUNKS):
-            order = range(PASSES) if c < EARLY_CHUNKS else reversed(range(PASSES))
-            for i, z in enumerate(order):
-                w1_passes(z, c, i == 0)
+            copies[0 if c == 1 else 1](h_rounded[c][:], h_bank[c][:].rearrange("p t s -> p s t"))
+        last_banks = [ps.tile([P, CHUNK], F32, name=name) for name in ("out_bank3", "h_bank0")]
+        out_part.append([bank[:] for bank in last_banks])
+
+        def adapter(c):
             nc.vector.quantize_mx(
                 out=h_codes[c][:].bitcast(FP8X4),
                 scales=h_plane[c][:],
@@ -195,15 +190,32 @@ def tile_picked_phlora_none_p_kernel(
             )
             for m in range(M_TILES):
                 nc.tensor.matmul_mx(
-                    out=out_bank[c][:, m, :],
+                    out=out_part[c][m],
                     lhsT=w3_codes[:, 2 * m * P : 2 * (m + 1) * P].bitcast(FP4X4),
                     lhsT_scale=w_plane[:, m, N : N + P],
                     rhs=h_codes[c][:].bitcast(FP8X4),
                     rhs_scale=h_plane[c][:],
                     start=False,
-                    stop=(m == M_TILES - 1),
+                    stop=(m == M_TILES - 1 or c == CHUNKS - 1),
                 )
-        for c in range(CHUNKS):
+
+        w1_passes(0, 0)
+        w1_passes(0, 1)
+        w1_passes(1, 0)
+        w1_passes(1, 1)
+        adapter(0)
+        adapter(1)
+        w1_passes(2, 0)
+        w1_passes(2, 1)
+        adapter(2)
+        w1_passes(3, 0)
+        w1_passes(3, 1)
+        adapter(3)
+        for c in range(CHUNKS - 1):
             result = sb.tile([P, M_TILES, CHUNK], F32, name="result%d" % c)
-            out_copy[c](result[:], out_bank[c][:])
+            copies[(c + 1) % 2](result[:], out_bank[c][:])
             nc.sync.dma_start(out_rows[:, :, c * CHUNK : (c + 1) * CHUNK], result[:])
+        for m in range(M_TILES):
+            result = sb.tile([P, CHUNK], F32, name="result_last%d" % m)
+            copies[m](result[:], last_banks[m][:])
+            nc.sync.dma_start(out_rows[:, m, S - CHUNK : S], result[:])

@@ -18,13 +18,13 @@ P = 128
 PACK = 4
 K_PASS = P * PACK
 PASSES = K // K_PASS
+QUAD = 32
+ROWS = 4
 CHUNK = 128
 CHUNKS = S // CHUNK
 GATHER = 256
 M_TILES = N // P
-HALF = P // 2
 SCALAR_SHARE = (64, 44)
-QUADRANTS = (0, 2, 1, 3)
 
 
 def tile_picked_phlora_none_p_kernel(
@@ -33,83 +33,75 @@ def tile_picked_phlora_none_p_kernel(
     nc = tc.nc
     with ExitStack() as ctx:
         sb = ctx.enter_context(tc.tile_pool(name="sb", bufs=1))
-        shared = ctx.enter_context(tc.tile_pool(name="shared", bufs=1))
-        early = ctx.enter_context(tc.tile_pool(name="early", bufs=1))
+        late = ctx.enter_context(tc.tile_pool(name="late", bufs=1))
         ps = ctx.enter_context(tc.psum_pool(name="ps", bufs=1))
+
+        def words(ap):
+            return ap.bitcast(I32)
 
         offsets = sb.tile([P, S // 16], U16, name="offsets")
         nc.sync.dma_start(offsets[:], offs)
 
-        byte_window = shared.tile([P, T], U8, name="byte_window", offset=4 * T - 64, align_bytes=64)
-        nc.vector.memset(byte_window[:].bitcast(I32), 0)
-        nc.sync.dma_start(
-            byte_window[0:P:4, :].bitcast(I32), x_scales.rearrange("z q c -> q z c").bitcast(I32)
-        )
-        x_plane = sb.tile([P, PASSES * S], U8, name="x_plane", align_bytes=64)
-        nc.vector.memset(x_plane[:].bitcast(I32), 0)
+        w_rows = sb.tile([P, 3 * N], U8, name="w_rows", align_bytes=64)
+        nc.vector.memset(words(w_rows[:]), 0)
+        byte_window = sb.tile([P, T], U8, name="byte_window", align_bytes=64)
+        nc.vector.memset(words(byte_window[:]), 0)
+        nc.sync.dma_start(words(w_rows[0:P:8, 0 : 2 * N]), words(w1_scales.rearrange("z q n -> q z n")))
+        nc.sync.dma_start(words(byte_window[0:P:4, :]), words(x_scales.rearrange("z q c -> q z c")))
+        nc.sync.dma_start(words(w_rows[0:P:8, 2 * N : 3 * N]), words(w3_scales[0]))
+        x_plane = [sb.tile([P, S], U8, name="x_plane%d" % z, align_bytes=64) for z in range(PASSES)]
+        nc.vector.memset(words(x_plane[1][:]), 0)
 
-        w_rows = sb.tile([P, N + P], U8, name="w_rows", align_bytes=64)
-        nc.sync.dma_start(w_rows[0:P:4, 0:N].bitcast(I32), w1_scales.rearrange("z q n -> q z n").bitcast(I32))
-        nc.sync.dma_start(
-            w_rows[0:P:4, N : N + P].bitcast(I32), w3_scales[0].rearrange("q (m n) -> (q m) n", n=P).bitcast(I32)
-        )
-
-        w2_first = early.tile([P, PACK, H], F32, name="w2_first", offset=0, align_bytes=64)
-        w2_first_rows = w2[0:K_PASS, :].rearrange("(p j) c -> p j c", j=PACK)
-        nc.scalar.dma_start(w2_first[:], w2_first_rows)
+        w2_raw = [sb.tile([P, PACK, H], F32, name="w2_raw%d" % z, align_bytes=64) for z in range(PASSES)]
+        w2_rows = w2.rearrange("(z p j) c -> z p j c", z=PASSES, j=PACK)
+        x_rows = x_words.rearrange("z p c r -> z p (c r)")
+        nc.scalar.dma_start(w2_raw[0][:], w2_rows[0])
         word_window = [sb.tile([P, T], I32, name="word_window0")]
-        nc.sync.dma_start(word_window[0][:], x_words[0].rearrange("p c r -> p (c r)").bitcast(I32))
-        w2_last_rows = w2[K_PASS:K, :].rearrange("(p j) c -> p j c", j=PACK)
-        w2_last = [sb.tile([P, 3, H], F32, name="w2_last0")]
-        nc.sync.dma_start(w2_last[0][:], w2_last_rows[:, 0:3, :])
+        nc.sync.dma_start(word_window[0][:], words(x_rows[0]))
+        nc.sync.dma_start(w2_raw[1][:], w2_rows[1])
 
-        picked_bytes = sb.tile([P, S], U8, name="picked_bytes", align_bytes=64)
-        nc.vector.tensor_copy(picked_bytes[:], byte_window[:].indirect(offsets[:]))
-        for q in QUADRANTS:
-            nc.sync.dma_start(
-                x_plane[32 * q : 32 * q + 4, :].bitcast(I32).rearrange("p (z s) -> p z s", z=PASSES),
-                picked_bytes[32 * q : 32 * q + 32 : 4, :].bitcast(I32),
-            )
+        held = 4 * T - 64
+        picked = late.tile([P, S + 9 * N], U8, name="picked", offset=held, align_bytes=64)
+        nc.vector.tensor_copy(picked[:, 0:S], byte_window[:].indirect(offsets[:]))
+        nc.vector.tensor_copy(words(x_plane[0][:]), words(picked[:, 0:S]))
+        for r in range(1, ROWS):
+            nc.sync.dma_start(words(x_plane[0][r:P:QUAD, :]), words(x_plane[0][8 * r : P : QUAD, :]))
 
-        w2_last.append(shared.tile([P, 1, H], F32, name="w2_last1", offset=4 * T + 1920, align_bytes=64))
-        nc.sync.dma_start(w2_last[1][:], w2_last_rows[:, 3:4, :])
-        word_window.append(shared.tile([P, T], I32, name="word_window1", offset=0, align_bytes=64))
-        nc.sync.dma_start(word_window[1][:], x_words[1].rearrange("p c r -> p (c r)").bitcast(I32))
-        w_plane = shared.tile([P, 2, N + P], U8, name="w_plane", offset=4 * T, align_bytes=64)
-        nc.vector.memset(w_plane[:].bitcast(I32), 0)
-        w1_codes = shared.tile([P, PASSES, 2 * N], U8, name="w1_codes", offset=4 * T + 768, align_bytes=64)
-        nc.sync.dma_start(w1_codes[:].bitcast(I32), w1_words.rearrange("z p n -> p z n").bitcast(I32))
+        word_window.append(late.tile([P, T], I32, name="word_window1", offset=0, align_bytes=64))
+        nc.sync.dma_start(word_window[1][:], words(x_rows[1]))
+        for r in range(ROWS):
+            nc.sync.dma_start(words(x_plane[1][r:P:QUAD, :]), words(x_plane[0][8 * r + 4 : P : QUAD, :]))
+
+        w1_codes = late.tile([P, PASSES, 2 * N], U8, name="w1_codes", offset=held + S, align_bytes=64)
+        nc.sync.dma_start(words(w1_codes[:]), words(w1_words.rearrange("z p n -> p z n")))
+        w3_codes = late.tile([P, 2 * N], U8, name="w3_codes", offset=held + S + 4 * N, align_bytes=64)
+        nc.sync.dma_start(words(w3_codes[:]), words(w3_words[0]))
+        w_plane = late.tile([P, 3 * N], U8, name="w_plane", offset=held + S + 6 * N, align_bytes=64)
+        nc.vector.tensor_copy(words(w_plane[:]), words(w_rows[:]))
+        for r in range(1, ROWS):
+            nc.sync.dma_start(words(w_plane[r:P:QUAD, :]), words(w_rows[8 * r : P : QUAD, :]))
 
         w2_codes = [sb.tile([P, H], U32, name="w2_codes%d" % z, align_bytes=64) for z in range(PASSES)]
         w2_plane = [sb.tile([P, H], U8, name="w2_plane%d" % z, align_bytes=64) for z in range(PASSES)]
-
-        def deal(copy, grouped, raw, m0, m1, j0=0, j1=PACK):
-            copy(
-                grouped[:, :, m0:m1, j0:j1].rearrange("p t m j -> p m j t"),
-                raw.rearrange("p j (m t) -> p m j t", t=PACK)[:, m0:m1, j0:j1, :],
-            )
-
-        grouped_first = sb.tile([P, PACK, P, PACK], BF16, name="grouped_first", align_bytes=64)
-        deal(nc.scalar.copy, grouped_first, w2_first[:], 0, SCALAR_SHARE[0])
-        deal(nc.vector.tensor_copy, grouped_first, w2_first[:], SCALAR_SHARE[0], P)
-        nc.vector.quantize_mx(
-            out=w2_codes[0][:].bitcast(FP8X4),
-            scales=w2_plane[0][:],
-            in_=grouped_first[:].rearrange("p t m j -> p (t m j)"),
-        )
-
-        w3_codes = early.tile([P, 2 * N], U8, name="w3_codes", offset=0, align_bytes=64)
-        nc.sync.dma_start(w3_codes[:].bitcast(I32), w3_words[0].bitcast(I32))
-        for q in QUADRANTS:
-            nc.sync.dma_start(
-                w_plane[32 * q : 32 * q + 4, :, :].bitcast(I32),
-                w_rows[32 * q : 32 * q + 32 : 4, :].bitcast(I32),
-            )
-
         x_codes = [
             [sb.tile([P, GATHER], U32, name="x_codes%d_%d" % (z, g), align_bytes=64) for g in range(S // GATHER)]
             for z in range(PASSES)
         ]
+        h_bank = [ps.tile([P, PACK, CHUNK], F32, name="h_bank%d" % c) for c in range(CHUNKS)]
+
+        def quantise_w2(z):
+            grouped = sb.tile([P, PACK, P, PACK], BF16, name="w2_grouped%d" % z, align_bytes=64)
+            share = SCALAR_SHARE[z]
+            for copy, m0, m1 in ((nc.scalar.copy, 0, share), (nc.vector.tensor_copy, share, P)):
+                copy(
+                    grouped[:, :, m0:m1, :].rearrange("p t m j -> p m j t"),
+                    w2_raw[z][:].rearrange("p j (m t) -> p m j t", t=PACK)[:, m0:m1, :, :],
+                )
+            nc.vector.quantize_mx(
+                out=w2_codes[z][:].bitcast(FP8X4),
+                scales=w2_plane[z][:],
+                in_=grouped[:].rearrange("p t m j -> p (t m j)"),
+            )
 
         def gather_words(z):
             for g in range(S // GATHER):
@@ -118,13 +110,9 @@ def tile_picked_phlora_none_p_kernel(
                     word_window[z][:].bitcast(U32).indirect(offsets[:, g * GATHER // 16 : (g + 1) * GATHER // 16]),
                 )
 
-        h_bank = [ps.tile([P, PACK, CHUNK], F32, name="h_bank%d" % c) for c in range(CHUNKS)]
-        out_bank = [ps.tile([P, M_TILES, CHUNK], F32, name="out_bank%d" % c) for c in range(CHUNKS - 1)]
-        out_part = [[out_bank[c][:, m, :] for m in range(M_TILES)] for c in range(CHUNKS - 1)]
-
         def x_operand(z, c):
             g, first = divmod(c * CHUNK, GATHER)
-            return x_codes[z][g][:, first : first + CHUNK].bitcast(FP8X4), x_plane[:, z * S + c * CHUNK : z * S + (c + 1) * CHUNK]
+            return x_codes[z][g][:, first : first + CHUNK].bitcast(FP8X4), x_plane[z][:, c * CHUNK : (c + 1) * CHUNK]
 
         def h_passes(z, c):
             rhs, rhs_scale = x_operand(z, c)
@@ -139,48 +127,37 @@ def tile_picked_phlora_none_p_kernel(
                     stop=(z == PASSES - 1 and t == PACK - 1),
                 )
 
-        def w1_passes(c, z):
-            rhs, rhs_scale = x_operand(z, c)
-            for m in range(M_TILES):
-                nc.tensor.matmul_mx(
-                    out=out_part[c][m],
-                    lhsT=w1_codes[:, z, 2 * m * P : 2 * (m + 1) * P].bitcast(FP4X4),
-                    lhsT_scale=w_plane[:, z, m * P : (m + 1) * P],
-                    rhs=rhs,
-                    rhs_scale=rhs_scale,
-                    start=(z == 0 and (m == 0 or c == CHUNKS - 1)),
-                    stop=False,
-                )
-
-        gather_words(0)
-        for c in range(CHUNKS):
-            h_passes(0, c)
-        grouped_last = sb.tile([P, PACK, P, PACK], BF16, name="grouped_last", align_bytes=64)
-        for u, (j0, j1) in enumerate(((0, 3), (3, PACK))):
-            for copy, m0, m1 in ((nc.scalar.copy, 0, SCALAR_SHARE[1]), (nc.vector.tensor_copy, SCALAR_SHARE[1], P)):
-                copy(
-                    grouped_last[:, :, m0:m1, j0:j1].rearrange("p t m j -> p m j t"),
-                    w2_last[u][:].rearrange("p j (m t) -> p m j t", t=PACK)[:, m0:m1, :, :],
-                )
-        nc.vector.quantize_mx(
-            out=w2_codes[1][:].bitcast(FP8X4),
-            scales=w2_plane[1][:],
-            in_=grouped_last[:].rearrange("p t m j -> p (t m j)"),
-        )
-
-        gather_words(1)
-        for c in range(CHUNKS):
-            h_passes(1, c)
+        for z in range(PASSES):
+            quantise_w2(z)
+            gather_words(z)
+            for c in range(CHUNKS):
+                h_passes(z, c)
 
         h_codes = [sb.tile([P, CHUNK], U32, name="h_codes%d" % c, align_bytes=64) for c in range(CHUNKS)]
         h_plane = [sb.tile([P, CHUNK], U8, name="h_plane%d" % c, align_bytes=64) for c in range(CHUNKS)]
         h_rounded = [sb.tile([P, CHUNK, PACK], BF16, name="h_rounded%d" % c, align_bytes=64) for c in range(CHUNKS)]
-        out_rows = out.rearrange("(m p) s -> p m s", p=P)
         copies = (nc.vector.tensor_copy, nc.scalar.copy)
         for c in range(CHUNKS):
             copies[0 if c == 1 else 1](h_rounded[c][:], h_bank[c][:].rearrange("p t s -> p s t"))
+
+        out_bank = [ps.tile([P, M_TILES, CHUNK], F32, name="out_bank%d" % c) for c in range(CHUNKS - 1)]
+        out_part = [[out_bank[c][:, m, :] for m in range(M_TILES)] for c in range(CHUNKS - 1)]
         last_banks = [ps.tile([P, CHUNK], F32, name=name) for name in ("out_bank3", "h_bank0")]
         out_part.append([bank[:] for bank in last_banks])
+
+        def w1_passes(c):
+            for z in range(PASSES):
+                rhs, rhs_scale = x_operand(z, c)
+                for m in range(M_TILES):
+                    nc.tensor.matmul_mx(
+                        out=out_part[c][m],
+                        lhsT=w1_codes[:, z, 2 * m * P : 2 * (m + 1) * P].bitcast(FP4X4),
+                        lhsT_scale=w_plane[:, z * N + m * P : z * N + (m + 1) * P],
+                        rhs=rhs,
+                        rhs_scale=rhs_scale,
+                        start=(z == 0 and (m == 0 or c == CHUNKS - 1)),
+                        stop=False,
+                    )
 
         def adapter(c):
             nc.vector.quantize_mx(
@@ -192,30 +169,28 @@ def tile_picked_phlora_none_p_kernel(
                 nc.tensor.matmul_mx(
                     out=out_part[c][m],
                     lhsT=w3_codes[:, 2 * m * P : 2 * (m + 1) * P].bitcast(FP4X4),
-                    lhsT_scale=w_plane[:, m, N : N + P],
+                    lhsT_scale=w_plane[:, 2 * N + m * P : 2 * N + (m + 1) * P],
                     rhs=h_codes[c][:].bitcast(FP8X4),
                     rhs_scale=h_plane[c][:],
                     start=False,
                     stop=(m == M_TILES - 1 or c == CHUNKS - 1),
                 )
 
-        w1_passes(0, 0)
-        w1_passes(0, 1)
-        w1_passes(1, 0)
-        w1_passes(1, 1)
+        w1_passes(0)
+        w1_passes(1)
         adapter(0)
         adapter(1)
-        w1_passes(2, 0)
-        w1_passes(2, 1)
+        w1_passes(2)
         adapter(2)
-        w1_passes(3, 0)
-        w1_passes(3, 1)
+        w1_passes(3)
         adapter(3)
-        for c in range(CHUNKS - 1):
+
+        out_rows = out.rearrange("(m p) s -> p m s", p=P)
+        for c in range(CHUNKS):
             result = sb.tile([P, M_TILES, CHUNK], F32, name="result%d" % c)
-            copies[(c + 1) % 2](result[:], out_bank[c][:])
+            if c < CHUNKS - 1:
+                copies[(c + 1) % 2](result[:], out_bank[c][:])
+            else:
+                for m in range(M_TILES):
+                    copies[m](result[:, m, :], last_banks[m][:])
             nc.sync.dma_start(out_rows[:, :, c * CHUNK : (c + 1) * CHUNK], result[:])
-        for m in range(M_TILES):
-            result = sb.tile([P, CHUNK], F32, name="result_last%d" % m)
-            copies[m](result[:], last_banks[m][:])
-            nc.sync.dma_start(out_rows[:, m, S - CHUNK : S], result[:])

@@ -83,10 +83,7 @@ def tile_picked_phlora_none_p_kernel(
 
         w2_codes = [sb.tile([P, H], U32, name="w2_codes%d" % z, align_bytes=64) for z in range(PASSES)]
         w2_plane = [sb.tile([P, H], U8, name="w2_plane%d" % z, align_bytes=64) for z in range(PASSES)]
-        x_codes = [
-            [sb.tile([P, GATHER], U32, name="x_codes%d_%d" % (z, g), align_bytes=64) for g in range(S // GATHER)]
-            for z in range(PASSES)
-        ]
+        x_codes = [sb.tile([P, S], U32, name="x_codes%d" % z, align_bytes=64) for z in range(PASSES)]
         h_bank = [ps.tile([P, PACK, CHUNK], F32, name="h_bank%d" % c) for c in range(CHUNKS)]
 
         def quantise_w2(z):
@@ -106,16 +103,16 @@ def tile_picked_phlora_none_p_kernel(
         def gather_words(z):
             for g in range(S // GATHER):
                 nc.vector.tensor_copy(
-                    x_codes[z][g][:],
+                    x_codes[z][:, g * GATHER : (g + 1) * GATHER],
                     word_window[z][:].bitcast(U32).indirect(offsets[:, g * GATHER // 16 : (g + 1) * GATHER // 16]),
                 )
 
-        def x_operand(z, c):
-            g, first = divmod(c * CHUNK, GATHER)
-            return x_codes[z][g][:, first : first + CHUNK].bitcast(FP8X4), x_plane[z][:, c * CHUNK : (c + 1) * CHUNK]
+        def x_operand(z, c0, c1):
+            places = slice(c0 * CHUNK, c1 * CHUNK)
+            return x_codes[z][:, places].bitcast(FP8X4), x_plane[z][:, places]
 
         def h_passes(z, c):
-            rhs, rhs_scale = x_operand(z, c)
+            rhs, rhs_scale = x_operand(z, c, c + 1)
             for t in range(PACK):
                 nc.tensor.matmul_mx(
                     out=h_bank[c][:, t, :],
@@ -140,24 +137,25 @@ def tile_picked_phlora_none_p_kernel(
         for c in range(CHUNKS):
             copies[0 if c == 1 else 1](h_rounded[c][:], h_bank[c][:].rearrange("p t s -> p s t"))
 
-        out_bank = [ps.tile([P, M_TILES, CHUNK], F32, name="out_bank%d" % c) for c in range(CHUNKS - 1)]
-        out_part = [[out_bank[c][:, m, :] for m in range(M_TILES)] for c in range(CHUNKS - 1)]
-        last_banks = [ps.tile([P, CHUNK], F32, name=name) for name in ("out_bank3", "h_bank0")]
+        first_bank = ps.tile([P, M_TILES, CHUNK], F32, name="first_bank")
+        middle_banks = [ps.tile([P, 2 * CHUNK], F32, name="middle_bank%d" % m) for m in range(M_TILES)]
+        last_banks = [ps.tile([P, CHUNK], F32, name=name) for name in ("last_bank", "h_bank0")]
+        out_part = [[first_bank[:, m, :] for m in range(M_TILES)]]
+        out_part.extend([bank[:, u * CHUNK : (u + 1) * CHUNK] for bank in middle_banks] for u in range(2))
         out_part.append([bank[:] for bank in last_banks])
 
-        def w1_passes(c):
-            for z in range(PASSES):
-                rhs, rhs_scale = x_operand(z, c)
-                for m in range(M_TILES):
-                    nc.tensor.matmul_mx(
-                        out=out_part[c][m],
-                        lhsT=w1_codes[:, z, 2 * m * P : 2 * (m + 1) * P].bitcast(FP4X4),
-                        lhsT_scale=w_plane[:, z * N + m * P : z * N + (m + 1) * P],
-                        rhs=rhs,
-                        rhs_scale=rhs_scale,
-                        start=(z == 0 and (m == 0 or c == CHUNKS - 1)),
-                        stop=False,
-                    )
+        def w1_passes(parts, c0, c1, z):
+            rhs, rhs_scale = x_operand(z, c0, c1)
+            for m in range(M_TILES):
+                nc.tensor.matmul_mx(
+                    out=parts[m],
+                    lhsT=w1_codes[:, z, 2 * m * P : 2 * (m + 1) * P].bitcast(FP4X4),
+                    lhsT_scale=w_plane[:, z * N + m * P : z * N + (m + 1) * P],
+                    rhs=rhs,
+                    rhs_scale=rhs_scale,
+                    start=(z == 0 and (m == 0 or c0 > 0)),
+                    stop=False,
+                )
 
         def adapter(c):
             nc.vector.quantize_mx(
@@ -173,24 +171,30 @@ def tile_picked_phlora_none_p_kernel(
                     rhs=h_codes[c][:].bitcast(FP8X4),
                     rhs_scale=h_plane[c][:],
                     start=False,
-                    stop=(m == M_TILES - 1 or c == CHUNKS - 1),
+                    stop=(c >= 2 or (c == 0 and m == M_TILES - 1)),
                 )
 
-        w1_passes(0)
-        w1_passes(1)
+        middle_part = [bank[:] for bank in middle_banks]
+        w1_passes(out_part[0], 0, 1, 0)
+        w1_passes(out_part[0], 0, 1, 1)
+        w1_passes(middle_part, 1, 3, 0)
         adapter(0)
+        w1_passes(middle_part, 1, 3, 1)
         adapter(1)
-        w1_passes(2)
         adapter(2)
-        w1_passes(3)
+        w1_passes(out_part[3], 3, 4, 0)
+        w1_passes(out_part[3], 3, 4, 1)
         adapter(3)
 
         out_rows = out.rearrange("(m p) s -> p m s", p=P)
-        for c in range(CHUNKS):
-            result = sb.tile([P, M_TILES, CHUNK], F32, name="result%d" % c)
-            if c < CHUNKS - 1:
-                copies[(c + 1) % 2](result[:], out_bank[c][:])
-            else:
-                for m in range(M_TILES):
-                    copies[m](result[:, m, :], last_banks[m][:])
-            nc.sync.dma_start(out_rows[:, :, c * CHUNK : (c + 1) * CHUNK], result[:])
+        first = sb.tile([P, M_TILES, CHUNK], F32, name="first_result")
+        nc.scalar.copy(first[:], first_bank[:])
+        nc.sync.dma_start(out_rows[:, :, 0:CHUNK], first[:])
+        middle = sb.tile([P, M_TILES, 2 * CHUNK], F32, name="middle_result")
+        for m in range(M_TILES):
+            copies[m](middle[:, m, :], middle_banks[m][:])
+        nc.sync.dma_start(out_rows[:, :, CHUNK : 3 * CHUNK], middle[:])
+        for m in range(M_TILES):
+            last = sb.tile([P, CHUNK], F32, name="last_result%d" % m)
+            copies[m](last[:], last_banks[m][:])
+            nc.sync.dma_start(out_rows[:, m, S - CHUNK : S], last[:])

@@ -20,11 +20,15 @@ K_PASS = P * PACK
 PASSES = K // K_PASS
 QUAD = 32
 ROWS = 4
+BLOCK_ROWS = QUAD // ROWS
+PASS_STEP = BLOCK_ROWS // PASSES
 CHUNK = 128
 CHUNKS = S // CHUNK
 GATHER = 256
 M_TILES = N // P
+ALIGN = 64
 SCALAR_SHARE = (64, 44)
+VECTOR_BANK = 1
 
 
 def tile_picked_phlora_none_p_kernel(
@@ -42,17 +46,17 @@ def tile_picked_phlora_none_p_kernel(
         offsets = sb.tile([P, S // 16], U16, name="offsets")
         nc.sync.dma_start(offsets[:], offs)
 
-        w_rows = sb.tile([P, 3 * N], U8, name="w_rows", align_bytes=64)
+        w_rows = sb.tile([P, 3 * N], U8, name="w_rows", align_bytes=ALIGN)
         nc.vector.memset(words(w_rows[:]), 0)
-        byte_window = sb.tile([P, T], U8, name="byte_window", align_bytes=64)
+        byte_window = sb.tile([P, T], U8, name="byte_window", align_bytes=ALIGN)
         nc.vector.memset(words(byte_window[:]), 0)
-        nc.sync.dma_start(words(w_rows[0:P:8, 0 : 2 * N]), words(w1_scales.rearrange("z q n -> q z n")))
-        nc.sync.dma_start(words(byte_window[0:P:4, :]), words(x_scales.rearrange("z q c -> q z c")))
-        nc.sync.dma_start(words(w_rows[0:P:8, 2 * N : 3 * N]), words(w3_scales[0]))
-        x_plane = [sb.tile([P, S], U8, name="x_plane%d" % z, align_bytes=64) for z in range(PASSES)]
+        nc.sync.dma_start(words(w_rows[0:P:BLOCK_ROWS, 0 : 2 * N]), words(w1_scales.rearrange("z q n -> q z n")))
+        nc.sync.dma_start(words(byte_window[0:P:PASS_STEP, :]), words(x_scales.rearrange("z q c -> q z c")))
+        nc.sync.dma_start(words(w_rows[0:P:BLOCK_ROWS, 2 * N : 3 * N]), words(w3_scales[0]))
+        x_plane = [sb.tile([P, S], U8, name="x_plane%d" % z, align_bytes=ALIGN) for z in range(PASSES)]
         nc.vector.memset(words(x_plane[1][:]), 0)
 
-        w2_raw = [sb.tile([P, PACK, H], F32, name="w2_raw%d" % z, align_bytes=64) for z in range(PASSES)]
+        w2_raw = [sb.tile([P, PACK, H], F32, name="w2_raw%d" % z, align_bytes=ALIGN) for z in range(PASSES)]
         w2_rows = w2.rearrange("(z p j) c -> z p j c", z=PASSES, j=PACK)
         x_rows = x_words.rearrange("z p c r -> z p (c r)")
         nc.scalar.dma_start(w2_raw[0][:], w2_rows[0])
@@ -60,34 +64,39 @@ def tile_picked_phlora_none_p_kernel(
         nc.sync.dma_start(word_window[0][:], words(x_rows[0]))
         nc.sync.dma_start(w2_raw[1][:], w2_rows[1])
 
-        held = 4 * T - 64
-        picked = late.tile([P, S + 9 * N], U8, name="picked", offset=held, align_bytes=64)
-        nc.vector.tensor_copy(picked[:, 0:S], byte_window[:].indirect(offsets[:]))
-        nc.vector.tensor_copy(words(x_plane[0][:]), words(picked[:, 0:S]))
+        picked_at = 4 * T - ALIGN
+        w1_codes_at = picked_at + S
+        w3_codes_at = w1_codes_at + PASSES * 2 * N
+        w_plane_at = w3_codes_at + 2 * N
+        picked = late.tile([P, S], U8, name="picked", offset=picked_at, align_bytes=ALIGN)
+        nc.vector.tensor_copy(picked[:], byte_window[:].indirect(offsets[:]))
+        nc.vector.tensor_copy(words(x_plane[0][:]), words(picked[:]))
         for r in range(1, ROWS):
-            nc.sync.dma_start(words(x_plane[0][r:P:QUAD, :]), words(x_plane[0][8 * r : P : QUAD, :]))
+            nc.sync.dma_start(words(x_plane[0][r:P:QUAD, :]), words(x_plane[0][BLOCK_ROWS * r : P : QUAD, :]))
 
-        word_window.append(late.tile([P, T], I32, name="word_window1", offset=0, align_bytes=64))
+        word_window.append(late.tile([P, T], I32, name="word_window1", offset=0, align_bytes=ALIGN))
         nc.sync.dma_start(word_window[1][:], words(x_rows[1]))
         for r in range(ROWS):
-            nc.sync.dma_start(words(x_plane[1][r:P:QUAD, :]), words(x_plane[0][8 * r + 4 : P : QUAD, :]))
+            nc.sync.dma_start(
+                words(x_plane[1][r:P:QUAD, :]), words(x_plane[0][BLOCK_ROWS * r + PASS_STEP : P : QUAD, :])
+            )
 
-        w1_codes = late.tile([P, PASSES, 2 * N], U8, name="w1_codes", offset=held + S, align_bytes=64)
+        w1_codes = late.tile([P, PASSES, 2 * N], U8, name="w1_codes", offset=w1_codes_at, align_bytes=ALIGN)
         nc.sync.dma_start(words(w1_codes[:]), words(w1_words.rearrange("z p n -> p z n")))
-        w3_codes = late.tile([P, 2 * N], U8, name="w3_codes", offset=held + S + 4 * N, align_bytes=64)
+        w3_codes = late.tile([P, 2 * N], U8, name="w3_codes", offset=w3_codes_at, align_bytes=ALIGN)
         nc.sync.dma_start(words(w3_codes[:]), words(w3_words[0]))
-        w_plane = late.tile([P, 3 * N], U8, name="w_plane", offset=held + S + 6 * N, align_bytes=64)
+        w_plane = late.tile([P, 3 * N], U8, name="w_plane", offset=w_plane_at, align_bytes=ALIGN)
         nc.vector.tensor_copy(words(w_plane[:]), words(w_rows[:]))
         for r in range(1, ROWS):
-            nc.sync.dma_start(words(w_plane[r:P:QUAD, :]), words(w_rows[8 * r : P : QUAD, :]))
+            nc.sync.dma_start(words(w_plane[r:P:QUAD, :]), words(w_rows[BLOCK_ROWS * r : P : QUAD, :]))
 
-        w2_codes = [sb.tile([P, H], U32, name="w2_codes%d" % z, align_bytes=64) for z in range(PASSES)]
-        w2_plane = [sb.tile([P, H], U8, name="w2_plane%d" % z, align_bytes=64) for z in range(PASSES)]
-        x_codes = [sb.tile([P, S], U32, name="x_codes%d" % z, align_bytes=64) for z in range(PASSES)]
+        w2_codes = [sb.tile([P, H], U32, name="w2_codes%d" % z, align_bytes=ALIGN) for z in range(PASSES)]
+        w2_plane = [sb.tile([P, H], U8, name="w2_plane%d" % z, align_bytes=ALIGN) for z in range(PASSES)]
+        x_codes = [sb.tile([P, S], U32, name="x_codes%d" % z, align_bytes=ALIGN) for z in range(PASSES)]
         h_bank = [ps.tile([P, PACK, CHUNK], F32, name="h_bank%d" % c) for c in range(CHUNKS)]
 
         def quantise_w2(z):
-            grouped = sb.tile([P, PACK, P, PACK], BF16, name="w2_grouped%d" % z, align_bytes=64)
+            grouped = sb.tile([P, PACK, P, PACK], BF16, name="w2_grouped%d" % z, align_bytes=ALIGN)
             share = SCALAR_SHARE[z]
             for copy, m0, m1 in ((nc.scalar.copy, 0, share), (nc.vector.tensor_copy, share, P)):
                 copy(
@@ -130,12 +139,12 @@ def tile_picked_phlora_none_p_kernel(
             for c in range(CHUNKS):
                 h_passes(z, c)
 
-        h_codes = [sb.tile([P, CHUNK], U32, name="h_codes%d" % c, align_bytes=64) for c in range(CHUNKS)]
-        h_plane = [sb.tile([P, CHUNK], U8, name="h_plane%d" % c, align_bytes=64) for c in range(CHUNKS)]
-        h_rounded = [sb.tile([P, CHUNK, PACK], BF16, name="h_rounded%d" % c, align_bytes=64) for c in range(CHUNKS)]
-        copies = (nc.vector.tensor_copy, nc.scalar.copy)
+        h_codes = [sb.tile([P, CHUNK], U32, name="h_codes%d" % c, align_bytes=ALIGN) for c in range(CHUNKS)]
+        h_plane = [sb.tile([P, CHUNK], U8, name="h_plane%d" % c, align_bytes=ALIGN) for c in range(CHUNKS)]
+        h_rounded = [sb.tile([P, CHUNK, PACK], BF16, name="h_rounded%d" % c, align_bytes=ALIGN) for c in range(CHUNKS)]
         for c in range(CHUNKS):
-            copies[0 if c == 1 else 1](h_rounded[c][:], h_bank[c][:].rearrange("p t s -> p s t"))
+            copy = nc.vector.tensor_copy if c == VECTOR_BANK else nc.scalar.copy
+            copy(h_rounded[c][:], h_bank[c][:].rearrange("p t s -> p s t"))
 
         first_bank = ps.tile([P, M_TILES, CHUNK], F32, name="first_bank")
         middle_banks = [ps.tile([P, 2 * CHUNK], F32, name="middle_bank%d" % m) for m in range(M_TILES)]
@@ -143,6 +152,7 @@ def tile_picked_phlora_none_p_kernel(
         out_part = [[first_bank[:, m, :] for m in range(M_TILES)]]
         out_part.extend([bank[:, u * CHUNK : (u + 1) * CHUNK] for bank in middle_banks] for u in range(2))
         out_part.append([bank[:] for bank in last_banks])
+        closes_bank = ((False, True), (False, False), (True, True), (True, True))
 
         def w1_passes(parts, c0, c1, z):
             rhs, rhs_scale = x_operand(z, c0, c1)
@@ -171,7 +181,7 @@ def tile_picked_phlora_none_p_kernel(
                     rhs=h_codes[c][:].bitcast(FP8X4),
                     rhs_scale=h_plane[c][:],
                     start=False,
-                    stop=(c >= 2 or (c == 0 and m == M_TILES - 1)),
+                    stop=closes_bank[c][m],
                 )
 
         middle_part = [bank[:] for bank in middle_banks]
@@ -186,6 +196,7 @@ def tile_picked_phlora_none_p_kernel(
         w1_passes(out_part[3], 3, 4, 1)
         adapter(3)
 
+        copies = (nc.vector.tensor_copy, nc.scalar.copy)
         out_rows = out.rearrange("(m p) s -> p m s", p=P)
         first = sb.tile([P, M_TILES, CHUNK], F32, name="first_result")
         nc.scalar.copy(first[:], first_bank[:])

@@ -27,6 +27,7 @@ CHUNKS = S // CHUNK
 GATHER = 256
 M_TILES = N // P
 ALIGN = 64
+BURST = 256
 SCALAR_SHARE = (64, 44)
 VECTOR_BANK = 1
 
@@ -48,7 +49,7 @@ def tile_picked_phlora_none_p_kernel(
 
         w_rows = sb.tile([P, 3 * N], U8, name="w_rows", align_bytes=ALIGN)
         nc.vector.memset(words(w_rows[:]), 0)
-        byte_window = sb.tile([P, T], U8, name="byte_window", align_bytes=ALIGN)
+        byte_window = sb.tile([P, T], U8, name="byte_window", align_bytes=BURST)
         nc.vector.memset(words(byte_window[:]), 0)
         nc.sync.dma_start(words(w_rows[0:P:BLOCK_ROWS, 0 : 2 * N]), words(w1_scales.rearrange("z q n -> q z n")))
         nc.sync.dma_start(words(byte_window[0:P:PASS_STEP, :]), words(x_scales.rearrange("z q c -> q z c")))
@@ -56,16 +57,16 @@ def tile_picked_phlora_none_p_kernel(
         x_plane = [sb.tile([P, S], U8, name="x_plane%d" % z, align_bytes=ALIGN) for z in range(PASSES)]
         nc.vector.memset(words(x_plane[1][:]), 0)
 
-        w2_raw = [sb.tile([P, PACK, H], F32, name="w2_raw%d" % z, align_bytes=ALIGN) for z in range(PASSES)]
+        w2_raw = [sb.tile([P, PACK, H], F32, name="w2_raw%d" % z, align_bytes=BURST) for z in range(PASSES)]
         w2_rows = w2.rearrange("(z p j) c -> z p j c", z=PASSES, j=PACK)
         x_rows = x_words.rearrange("z p c r -> z p (c r)")
         nc.scalar.dma_start(w2_raw[0][:], w2_rows[0])
-        word_window = [sb.tile([P, T], I32, name="word_window0")]
+        word_window = [sb.tile([P, T], I32, name="word_window0", align_bytes=BURST)]
         nc.sync.dma_start(word_window[0][:], words(x_rows[0]))
         nc.sync.dma_start(w2_raw[1][:], w2_rows[1])
 
         picked_at = 4 * T - ALIGN
-        w1_codes_at = picked_at + S
+        w1_codes_at = 4 * T + S
         w3_codes_at = w1_codes_at + PASSES * 2 * N
         w_plane_at = w3_codes_at + 2 * N
         picked = late.tile([P, S], U8, name="picked", offset=picked_at, align_bytes=ALIGN)
@@ -74,7 +75,7 @@ def tile_picked_phlora_none_p_kernel(
         for r in range(1, ROWS):
             nc.sync.dma_start(words(x_plane[0][r:P:QUAD, :]), words(x_plane[0][BLOCK_ROWS * r : P : QUAD, :]))
 
-        word_window.append(late.tile([P, T], I32, name="word_window1", offset=0, align_bytes=ALIGN))
+        word_window.append(late.tile([P, T], I32, name="word_window1", offset=0, align_bytes=BURST))
         nc.sync.dma_start(word_window[1][:], words(x_rows[1]))
         for r in range(ROWS):
             nc.sync.dma_start(
@@ -198,14 +199,14 @@ def tile_picked_phlora_none_p_kernel(
 
         copies = (nc.vector.tensor_copy, nc.scalar.copy)
         out_rows = out.rearrange("(m p) s -> p m s", p=P)
-        first = sb.tile([P, M_TILES, CHUNK], F32, name="first_result")
+        first = sb.tile([P, M_TILES, CHUNK], F32, name="first_result", align_bytes=BURST)
         nc.scalar.copy(first[:], first_bank[:])
         nc.sync.dma_start(out_rows[:, :, 0:CHUNK], first[:])
-        middle = sb.tile([P, M_TILES, 2 * CHUNK], F32, name="middle_result")
+        middle = sb.tile([P, M_TILES, 2 * CHUNK], F32, name="middle_result", align_bytes=BURST)
         for m in range(M_TILES):
             copies[m](middle[:, m, :], middle_banks[m][:])
         nc.sync.dma_start(out_rows[:, :, CHUNK : 3 * CHUNK], middle[:])
         for m in range(M_TILES):
-            last = sb.tile([P, CHUNK], F32, name="last_result%d" % m)
+            last = sb.tile([P, CHUNK], F32, name="last_result%d" % m, align_bytes=BURST)
             copies[m](last[:], last_banks[m][:])
             nc.sync.dma_start(out_rows[:, m, S - CHUNK : S], last[:])

@@ -47,15 +47,18 @@ def tile_picked_phlora_none_p_kernel(
         offsets = sb.tile([P, S // 16], U16, name="offsets")
         nc.sync.dma_start(offsets[:], offs)
 
-        w_rows = sb.tile([P, 3 * N], U8, name="w_rows", align_bytes=ALIGN)
-        nc.vector.memset(words(w_rows[:]), 0)
+        planes = sb.tile([P, S + 3 * N], U8, name="planes", align_bytes=ALIGN)
+        w_plane = planes[:, S : S + 3 * N]
+        early, rest = slice(0, S + N), slice(S + N, S + 3 * N)
+        nc.vector.memset(words(w_plane), 0)
         byte_window = sb.tile([P, T], U8, name="byte_window", align_bytes=BURST)
         nc.vector.memset(words(byte_window[:]), 0)
-        nc.sync.dma_start(words(w_rows[0:P:BLOCK_ROWS, 0 : 2 * N]), words(w1_scales.rearrange("z q n -> q z n")))
+        nc.sync.dma_start(words(planes[0:P:BLOCK_ROWS, S : S + 2 * N]), words(w1_scales.rearrange("z q n -> q z n")))
         nc.sync.dma_start(words(byte_window[0:P:PASS_STEP, :]), words(x_scales.rearrange("z q c -> q z c")))
-        nc.sync.dma_start(words(w_rows[0:P:BLOCK_ROWS, 2 * N : 3 * N]), words(w3_scales[0]))
-        x_plane = [sb.tile([P, S], U8, name="x_plane%d" % z, align_bytes=ALIGN) for z in range(PASSES)]
-        nc.vector.memset(words(x_plane[1][:]), 0)
+        nc.sync.dma_start(words(planes[0:P:BLOCK_ROWS, S + 2 * N : S + 3 * N]), words(w3_scales[0]))
+        late_plane = sb.tile([P, S], U8, name="late_plane", align_bytes=ALIGN)
+        nc.vector.memset(words(late_plane[:]), 0)
+        x_plane = [planes[:, 0:S], late_plane[:]]
 
         w2_raw = [sb.tile([P, PACK, H], F32, name="w2_raw%d" % z, align_bytes=BURST) for z in range(PASSES)]
         w2_rows = w2.rearrange("(z p j) c -> z p j c", z=PASSES, j=PACK)
@@ -68,28 +71,26 @@ def tile_picked_phlora_none_p_kernel(
         picked_at = 4 * T - ALIGN
         w1_codes_at = 4 * T + S
         w3_codes_at = w1_codes_at + PASSES * 2 * N
-        w_plane_at = w3_codes_at + 2 * N
         picked = late.tile([P, S], U8, name="picked", offset=picked_at, align_bytes=ALIGN)
         nc.vector.tensor_copy(picked[:], byte_window[:].indirect(offsets[:]))
-        nc.vector.tensor_copy(words(x_plane[0][:]), words(picked[:]))
+        nc.vector.tensor_copy(words(x_plane[0]), words(picked[:]))
         for r in range(1, ROWS):
-            nc.sync.dma_start(words(x_plane[0][r:P:QUAD, :]), words(x_plane[0][BLOCK_ROWS * r : P : QUAD, :]))
+            nc.sync.dma_start(words(planes[r:P:QUAD, early]), words(planes[BLOCK_ROWS * r : P : QUAD, early]))
 
         word_window.append(late.tile([P, T], I32, name="word_window1", offset=0, align_bytes=BURST))
         nc.sync.dma_start(word_window[1][:], words(x_rows[1]))
+        w1_codes = [
+            late.tile([P, 2 * N], U8, name="w1_codes%d" % z, offset=w1_codes_at + z * 2 * N, align_bytes=ALIGN)
+            for z in range(PASSES)
+        ]
+        nc.sync.dma_start(words(w1_codes[0][:]), words(w1_words[0]))
         for r in range(ROWS):
-            nc.sync.dma_start(
-                words(x_plane[1][r:P:QUAD, :]), words(x_plane[0][BLOCK_ROWS * r + PASS_STEP : P : QUAD, :])
-            )
-
-        w1_codes = late.tile([P, PASSES, 2 * N], U8, name="w1_codes", offset=w1_codes_at, align_bytes=ALIGN)
-        nc.sync.dma_start(words(w1_codes[:]), words(w1_words.rearrange("z p n -> p z n")))
+            nc.sync.dma_start(words(late_plane[r:P:QUAD, :]), words(planes[BLOCK_ROWS * r + PASS_STEP : P : QUAD, 0:S]))
+        nc.sync.dma_start(words(w1_codes[1][:]), words(w1_words[1]))
         w3_codes = late.tile([P, 2 * N], U8, name="w3_codes", offset=w3_codes_at, align_bytes=ALIGN)
         nc.sync.dma_start(words(w3_codes[:]), words(w3_words[0]))
-        w_plane = late.tile([P, 3 * N], U8, name="w_plane", offset=w_plane_at, align_bytes=ALIGN)
-        nc.vector.tensor_copy(words(w_plane[:]), words(w_rows[:]))
         for r in range(1, ROWS):
-            nc.sync.dma_start(words(w_plane[r:P:QUAD, :]), words(w_rows[BLOCK_ROWS * r : P : QUAD, :]))
+            nc.sync.dma_start(words(planes[r:P:QUAD, rest]), words(planes[BLOCK_ROWS * r : P : QUAD, rest]))
 
         w2_codes = [sb.tile([P, H], U32, name="w2_codes%d" % z, align_bytes=ALIGN) for z in range(PASSES)]
         w2_plane = [sb.tile([P, H], U8, name="w2_plane%d" % z, align_bytes=ALIGN) for z in range(PASSES)]
@@ -134,11 +135,34 @@ def tile_picked_phlora_none_p_kernel(
                     stop=(z == PASSES - 1 and t == PACK - 1),
                 )
 
+        first_bank = ps.tile([P, M_TILES, CHUNK], F32, name="first_bank")
+        middle_banks = [ps.tile([P, 2 * CHUNK], F32, name="middle_bank%d" % m) for m in range(M_TILES)]
+        out_part = [[first_bank[:, m, :] for m in range(M_TILES)]]
+        out_part.extend([bank[:, u * CHUNK : (u + 1) * CHUNK] for bank in middle_banks] for u in range(2))
+        closes_bank = ((False, True), (False, False), (True, True), (True, True))
+
+        def w1_passes(parts, c0, c1, z, opens):
+            rhs, rhs_scale = x_operand(z, c0, c1)
+            for m in range(M_TILES):
+                nc.tensor.matmul_mx(
+                    out=parts[m],
+                    lhsT=w1_codes[z][:, 2 * m * P : 2 * (m + 1) * P].bitcast(FP4X4),
+                    lhsT_scale=w_plane[:, z * N + m * P : z * N + (m + 1) * P],
+                    rhs=rhs,
+                    rhs_scale=rhs_scale,
+                    start=(opens and (m == 0 or c0 > 0)),
+                    stop=False,
+                )
+
+        middle_part = [bank[:] for bank in middle_banks]
         for z in range(PASSES):
             quantise_w2(z)
             gather_words(z)
             for c in range(CHUNKS):
                 h_passes(z, c)
+            if z == 0:
+                w1_passes(middle_part, 1, 3, 0, True)
+                w1_passes(out_part[0], 0, 1, 0, True)
 
         h_codes = [sb.tile([P, CHUNK], U32, name="h_codes%d" % c, align_bytes=ALIGN) for c in range(CHUNKS)]
         h_plane = [sb.tile([P, CHUNK], U8, name="h_plane%d" % c, align_bytes=ALIGN) for c in range(CHUNKS)]
@@ -146,27 +170,6 @@ def tile_picked_phlora_none_p_kernel(
         for c in range(CHUNKS):
             copy = nc.vector.tensor_copy if c == VECTOR_BANK else nc.scalar.copy
             copy(h_rounded[c][:], h_bank[c][:].rearrange("p t s -> p s t"))
-
-        first_bank = ps.tile([P, M_TILES, CHUNK], F32, name="first_bank")
-        middle_banks = [ps.tile([P, 2 * CHUNK], F32, name="middle_bank%d" % m) for m in range(M_TILES)]
-        last_banks = [ps.tile([P, CHUNK], F32, name=name) for name in ("last_bank", "h_bank0")]
-        out_part = [[first_bank[:, m, :] for m in range(M_TILES)]]
-        out_part.extend([bank[:, u * CHUNK : (u + 1) * CHUNK] for bank in middle_banks] for u in range(2))
-        out_part.append([bank[:] for bank in last_banks])
-        closes_bank = ((False, True), (False, False), (True, True), (True, True))
-
-        def w1_passes(parts, c0, c1, z):
-            rhs, rhs_scale = x_operand(z, c0, c1)
-            for m in range(M_TILES):
-                nc.tensor.matmul_mx(
-                    out=parts[m],
-                    lhsT=w1_codes[:, z, 2 * m * P : 2 * (m + 1) * P].bitcast(FP4X4),
-                    lhsT_scale=w_plane[:, z * N + m * P : z * N + (m + 1) * P],
-                    rhs=rhs,
-                    rhs_scale=rhs_scale,
-                    start=(z == 0 and (m == 0 or c0 > 0)),
-                    stop=False,
-                )
 
         def adapter(c):
             nc.vector.quantize_mx(
@@ -185,16 +188,15 @@ def tile_picked_phlora_none_p_kernel(
                     stop=closes_bank[c][m],
                 )
 
-        middle_part = [bank[:] for bank in middle_banks]
-        w1_passes(out_part[0], 0, 1, 0)
-        w1_passes(out_part[0], 0, 1, 1)
-        w1_passes(middle_part, 1, 3, 0)
+        last_banks = [ps.tile([P, CHUNK], F32, name=name) for name in ("last_bank", "h_bank0")]
+        out_part.append([bank[:] for bank in last_banks])
+        w1_passes(out_part[0], 0, 1, 1, False)
+        w1_passes(middle_part, 1, 3, 1, False)
         adapter(0)
-        w1_passes(middle_part, 1, 3, 1)
         adapter(1)
         adapter(2)
-        w1_passes(out_part[3], 3, 4, 0)
-        w1_passes(out_part[3], 3, 4, 1)
+        w1_passes(out_part[3], 3, 4, 1, True)
+        w1_passes(out_part[3], 3, 4, 0, False)
         adapter(3)
 
         copies = (nc.vector.tensor_copy, nc.scalar.copy)
@@ -206,7 +208,7 @@ def tile_picked_phlora_none_p_kernel(
         for m in range(M_TILES):
             copies[m](middle[:, m, :], middle_banks[m][:])
         nc.sync.dma_start(out_rows[:, :, CHUNK : 3 * CHUNK], middle[:])
+        last = sb.tile([P, M_TILES, CHUNK], F32, name="last_result", align_bytes=BURST)
         for m in range(M_TILES):
-            last = sb.tile([P, CHUNK], F32, name="last_result%d" % m, align_bytes=BURST)
-            copies[m](last[:], last_banks[m][:])
-            nc.sync.dma_start(out_rows[:, m, S - CHUNK : S], last[:])
+            copies[m](last[:, m, :], last_banks[m][:])
+        nc.sync.dma_start(out_rows[:, :, S - CHUNK : S], last[:])

@@ -47,18 +47,20 @@ def tile_picked_phlora_none_p_kernel(
         offsets = sb.tile([P, S // 16], U16, name="offsets")
         nc.sync.dma_start(offsets[:], offs)
 
-        planes = sb.tile([P, S + 3 * N], U8, name="planes", align_bytes=ALIGN)
-        w_plane = planes[:, S : S + 3 * N]
-        early, rest = slice(0, S + N), slice(S + N, S + 3 * N)
-        nc.vector.memset(words(w_plane), 0)
+        staged = sb.tile([P, S + 2 * N], U8, name="staged", align_bytes=ALIGN)
+        nc.vector.memset(words(staged[:, S : S + 2 * N]), 0)
         byte_window = sb.tile([P, T], U8, name="byte_window", align_bytes=BURST)
         nc.vector.memset(words(byte_window[:]), 0)
-        nc.sync.dma_start(words(planes[0:P:BLOCK_ROWS, S : S + 2 * N]), words(w1_scales.rearrange("z q n -> q z n")))
+        nc.sync.dma_start(words(staged[0:P:PASS_STEP, S : S + N]), words(w1_scales.rearrange("z q n -> q z n")))
         nc.sync.dma_start(words(byte_window[0:P:PASS_STEP, :]), words(x_scales.rearrange("z q c -> q z c")))
-        nc.sync.dma_start(words(planes[0:P:BLOCK_ROWS, S + 2 * N : S + 3 * N]), words(w3_scales[0]))
-        late_plane = sb.tile([P, S], U8, name="late_plane", align_bytes=ALIGN)
-        nc.vector.memset(words(late_plane[:]), 0)
-        x_plane = [planes[:, 0:S], late_plane[:]]
+        nc.sync.dma_start(words(staged[PASS_STEP:P:BLOCK_ROWS, S + N : S + 2 * N]), words(w3_scales[0]))
+        lowered = sb.tile([P, S + 2 * N], U8, name="lowered", align_bytes=ALIGN)
+        nc.vector.memset(words(lowered[:]), 0)
+        raised = sb.tile([P, S], U8, name="raised", align_bytes=ALIGN)
+        h_x_plane = [staged[:, 0:S], raised[PASS_STEP:P, :]]
+        w1_x_plane = [staged[:, 0:S], lowered[:, 0:S]]
+        w1_plane = [staged[:, S : S + N], lowered[:, S : S + N]]
+        w3_plane = lowered[:, S + N : S + 2 * N]
 
         w2_raw = [sb.tile([P, PACK, H], F32, name="w2_raw%d" % z, align_bytes=BURST) for z in range(PASSES)]
         w2_rows = w2.rearrange("(z p j) c -> z p j c", z=PASSES, j=PACK)
@@ -68,14 +70,15 @@ def tile_picked_phlora_none_p_kernel(
         nc.sync.dma_start(word_window[0][:], words(x_rows[0]))
         nc.sync.dma_start(w2_raw[1][:], w2_rows[1])
 
-        picked_at = 4 * T - ALIGN
+        picked_at = 4 * T
         w1_codes_at = 4 * T + S
         w3_codes_at = w1_codes_at + PASSES * 2 * N
         picked = late.tile([P, S], U8, name="picked", offset=picked_at, align_bytes=ALIGN)
         nc.vector.tensor_copy(picked[:], byte_window[:].indirect(offsets[:]))
-        nc.vector.tensor_copy(words(x_plane[0]), words(picked[:]))
+        nc.vector.tensor_copy(words(staged[:, 0:S]), words(picked[:]))
+        nc.vector.tensor_copy(words(raised[:]), words(picked[:]))
         for r in range(1, ROWS):
-            nc.sync.dma_start(words(planes[r:P:QUAD, early]), words(planes[BLOCK_ROWS * r : P : QUAD, early]))
+            nc.sync.dma_start(words(staged[r:P:QUAD, 0 : S + N]), words(staged[BLOCK_ROWS * r : P : QUAD, 0 : S + N]))
 
         word_window.append(late.tile([P, T], I32, name="word_window1", offset=0, align_bytes=BURST))
         nc.sync.dma_start(word_window[1][:], words(x_rows[1]))
@@ -84,13 +87,15 @@ def tile_picked_phlora_none_p_kernel(
             for z in range(PASSES)
         ]
         nc.sync.dma_start(words(w1_codes[0][:]), words(w1_words[0]))
-        for r in range(ROWS):
-            nc.sync.dma_start(words(late_plane[r:P:QUAD, :]), words(planes[BLOCK_ROWS * r + PASS_STEP : P : QUAD, 0:S]))
+        for r in range(1, ROWS):
+            nc.sync.dma_start(
+                words(raised[PASS_STEP + r : P : QUAD, :]), words(raised[PASS_STEP + BLOCK_ROWS * r : P : QUAD, :])
+            )
         nc.sync.dma_start(words(w1_codes[1][:]), words(w1_words[1]))
         w3_codes = late.tile([P, 2 * N], U8, name="w3_codes", offset=w3_codes_at, align_bytes=ALIGN)
         nc.sync.dma_start(words(w3_codes[:]), words(w3_words[0]))
-        for r in range(1, ROWS):
-            nc.sync.dma_start(words(planes[r:P:QUAD, rest]), words(planes[BLOCK_ROWS * r : P : QUAD, rest]))
+        for r in range(ROWS):
+            nc.sync.dma_start(words(lowered[r:P:QUAD, :]), words(staged[PASS_STEP + BLOCK_ROWS * r : P : QUAD, :]))
 
         w2_codes = [sb.tile([P, H], U32, name="w2_codes%d" % z, align_bytes=ALIGN) for z in range(PASSES)]
         w2_plane = [sb.tile([P, H], U8, name="w2_plane%d" % z, align_bytes=ALIGN) for z in range(PASSES)]
@@ -118,12 +123,12 @@ def tile_picked_phlora_none_p_kernel(
                     word_window[z][:].bitcast(U32).indirect(offsets[:, g * GATHER // 16 : (g + 1) * GATHER // 16]),
                 )
 
-        def x_operand(z, c0, c1):
+        def x_operand(z, c0, c1, x_plane):
             places = slice(c0 * CHUNK, c1 * CHUNK)
             return x_codes[z][:, places].bitcast(FP8X4), x_plane[z][:, places]
 
         def h_passes(z, c):
-            rhs, rhs_scale = x_operand(z, c, c + 1)
+            rhs, rhs_scale = x_operand(z, c, c + 1, h_x_plane)
             for t in range(PACK):
                 nc.tensor.matmul_mx(
                     out=h_bank[c][:, t, :],
@@ -142,12 +147,12 @@ def tile_picked_phlora_none_p_kernel(
         closes_bank = ((False, True), (False, False), (True, True), (True, True))
 
         def w1_passes(parts, c0, c1, z, opens):
-            rhs, rhs_scale = x_operand(z, c0, c1)
+            rhs, rhs_scale = x_operand(z, c0, c1, w1_x_plane)
             for m in range(M_TILES):
                 nc.tensor.matmul_mx(
                     out=parts[m],
                     lhsT=w1_codes[z][:, 2 * m * P : 2 * (m + 1) * P].bitcast(FP4X4),
-                    lhsT_scale=w_plane[:, z * N + m * P : z * N + (m + 1) * P],
+                    lhsT_scale=w1_plane[z][:, m * P : (m + 1) * P],
                     rhs=rhs,
                     rhs_scale=rhs_scale,
                     start=(opens and (m == 0 or c0 > 0)),
@@ -181,7 +186,7 @@ def tile_picked_phlora_none_p_kernel(
                 nc.tensor.matmul_mx(
                     out=out_part[c][m],
                     lhsT=w3_codes[:, 2 * m * P : 2 * (m + 1) * P].bitcast(FP4X4),
-                    lhsT_scale=w_plane[:, 2 * N + m * P : 2 * N + (m + 1) * P],
+                    lhsT_scale=w3_plane[:, m * P : (m + 1) * P],
                     rhs=h_codes[c][:].bitcast(FP8X4),
                     rhs_scale=h_plane[c][:],
                     start=False,

@@ -82,16 +82,12 @@ def tile_picked_phlora_none_p_kernel(
 
         word_window.append(late.tile([P, T], I32, name="word_window1", offset=0, align_bytes=BURST))
         nc.sync.dma_start(word_window[1][:], words(x_rows[1]))
-        w1_codes = [
-            late.tile([P, 2 * N], U8, name="w1_codes%d" % z, offset=w1_codes_at + z * 2 * N, align_bytes=ALIGN)
-            for z in range(PASSES)
-        ]
-        nc.sync.dma_start(words(w1_codes[0][:]), words(w1_words[0]))
         for r in range(1, ROWS):
             nc.sync.dma_start(
                 words(raised[PASS_STEP + r : P : QUAD, :]), words(raised[PASS_STEP + BLOCK_ROWS * r : P : QUAD, :])
             )
-        nc.sync.dma_start(words(w1_codes[1][:]), words(w1_words[1]))
+        w1_codes = late.tile([P, PASSES, 2 * N], U8, name="w1_codes", offset=w1_codes_at, align_bytes=ALIGN)
+        nc.sync.dma_start(words(w1_codes[:]), words(w1_words.rearrange("z p n -> p z n")))
         w3_codes = late.tile([P, 2 * N], U8, name="w3_codes", offset=w3_codes_at, align_bytes=ALIGN)
         nc.sync.dma_start(words(w3_codes[:]), words(w3_words[0]))
         for r in range(ROWS):
@@ -151,7 +147,7 @@ def tile_picked_phlora_none_p_kernel(
             for m in range(M_TILES):
                 nc.tensor.matmul_mx(
                     out=parts[m],
-                    lhsT=w1_codes[z][:, 2 * m * P : 2 * (m + 1) * P].bitcast(FP4X4),
+                    lhsT=w1_codes[:, z, 2 * m * P : 2 * (m + 1) * P].bitcast(FP4X4),
                     lhsT_scale=w1_plane[z][:, m * P : (m + 1) * P],
                     rhs=rhs,
                     rhs_scale=rhs_scale,
@@ -165,9 +161,6 @@ def tile_picked_phlora_none_p_kernel(
             gather_words(z)
             for c in range(CHUNKS):
                 h_passes(z, c)
-            if z == 0:
-                w1_passes(middle_part, 1, 3, 0, True)
-                w1_passes(out_part[0], 0, 1, 0, True)
 
         h_codes = [sb.tile([P, CHUNK], U32, name="h_codes%d" % c, align_bytes=ALIGN) for c in range(CHUNKS)]
         h_plane = [sb.tile([P, CHUNK], U8, name="h_plane%d" % c, align_bytes=ALIGN) for c in range(CHUNKS)]
@@ -195,9 +188,11 @@ def tile_picked_phlora_none_p_kernel(
 
         last_banks = [ps.tile([P, CHUNK], F32, name=name) for name in ("last_bank", "h_bank0")]
         out_part.append([bank[:] for bank in last_banks])
+        w1_passes(out_part[0], 0, 1, 0, True)
+        w1_passes(middle_part, 1, 3, 0, True)
         w1_passes(out_part[0], 0, 1, 1, False)
-        w1_passes(middle_part, 1, 3, 1, False)
         adapter(0)
+        w1_passes(middle_part, 1, 3, 1, False)
         adapter(1)
         adapter(2)
         w1_passes(out_part[3], 3, 4, 1, True)
@@ -213,7 +208,7 @@ def tile_picked_phlora_none_p_kernel(
         for m in range(M_TILES):
             copies[m](middle[:, m, :], middle_banks[m][:])
         nc.sync.dma_start(out_rows[:, :, CHUNK : 3 * CHUNK], middle[:])
-        last = sb.tile([P, M_TILES, CHUNK], F32, name="last_result", align_bytes=BURST)
         for m in range(M_TILES):
-            copies[m](last[:, m, :], last_banks[m][:])
-        nc.sync.dma_start(out_rows[:, :, S - CHUNK : S], last[:])
+            last = sb.tile([P, CHUNK], F32, name="last_result%d" % m, align_bytes=BURST)
+            copies[m](last[:], last_banks[m][:])
+            nc.sync.dma_start(out_rows[:, m, S - CHUNK : S], last[:])

@@ -48,12 +48,13 @@ def tile_picked_phlora_none_p_kernel(
         nc.sync.dma_start(offsets[:], offs)
 
         staged = sb.tile([P, S + 2 * N], U8, name="staged", align_bytes=ALIGN)
-        nc.vector.memset(words(staged[:, S : S + 2 * N]), 0)
+        nc.vector.memset(words(staged[:, S : S + N]), 0)
         byte_window = sb.tile([P, T], U8, name="byte_window", align_bytes=BURST)
         nc.vector.memset(words(byte_window[:]), 0)
         nc.sync.dma_start(words(staged[0:P:PASS_STEP, S : S + N]), words(w1_scales.rearrange("z q n -> q z n")))
         nc.sync.dma_start(words(byte_window[0:P:PASS_STEP, :]), words(x_scales.rearrange("z q c -> q z c")))
         nc.sync.dma_start(words(staged[PASS_STEP:P:BLOCK_ROWS, S + N : S + 2 * N]), words(w3_scales[0]))
+
         lowered = sb.tile([P, S + 2 * N], U8, name="lowered", align_bytes=ALIGN)
         nc.vector.memset(words(lowered[:]), 0)
         raised = sb.tile([P, S], U8, name="raised", align_bytes=ALIGN)
@@ -86,6 +87,7 @@ def tile_picked_phlora_none_p_kernel(
             nc.sync.dma_start(
                 words(raised[PASS_STEP + r : P : QUAD, :]), words(raised[PASS_STEP + BLOCK_ROWS * r : P : QUAD, :])
             )
+
         w1_codes = late.tile([P, PASSES, 2 * N], U8, name="w1_codes", offset=w1_codes_at, align_bytes=ALIGN)
         nc.sync.dma_start(words(w1_codes[:]), words(w1_words.rearrange("z p n -> p z n")))
         w3_codes = late.tile([P, 2 * N], U8, name="w3_codes", offset=w3_codes_at, align_bytes=ALIGN)

@@ -53,7 +53,6 @@ def tile_picked_phlora_none_p_kernel(
         nc.vector.memset(words(byte_window[:]), 0)
         nc.sync.dma_start(words(staged[0:P:PASS_STEP, S : S + N]), words(w1_scales.rearrange("z q n -> q z n")))
         nc.sync.dma_start(words(byte_window[0:P:PASS_STEP, :]), words(x_scales.rearrange("z q c -> q z c")))
-        nc.sync.dma_start(words(staged[PASS_STEP:P:BLOCK_ROWS, S + N : S + 2 * N]), words(w3_scales[0]))
 
         lowered = sb.tile([P, S + 2 * N], U8, name="lowered", align_bytes=ALIGN)
         nc.vector.memset(words(lowered[:]), 0)
@@ -88,6 +87,7 @@ def tile_picked_phlora_none_p_kernel(
                 words(raised[PASS_STEP + r : P : QUAD, :]), words(raised[PASS_STEP + BLOCK_ROWS * r : P : QUAD, :])
             )
 
+        nc.sync.dma_start(words(staged[PASS_STEP:P:BLOCK_ROWS, S + N : S + 2 * N]), words(w3_scales[0]))
         w1_codes = late.tile([P, PASSES, 2 * N], U8, name="w1_codes", offset=w1_codes_at, align_bytes=ALIGN)
         nc.sync.dma_start(words(w1_codes[:]), words(w1_words.rearrange("z p n -> p z n")))
         w3_codes = late.tile([P, 2 * N], U8, name="w3_codes", offset=w3_codes_at, align_bytes=ALIGN)

@@ -167,16 +167,23 @@ def tile_picked_phlora_none_p_kernel(
         h_codes = [sb.tile([P, CHUNK], U32, name="h_codes%d" % c, align_bytes=ALIGN) for c in range(CHUNKS)]
         h_plane = [sb.tile([P, CHUNK], U8, name="h_plane%d" % c, align_bytes=ALIGN) for c in range(CHUNKS)]
         h_rounded = [sb.tile([P, CHUNK, PACK], BF16, name="h_rounded%d" % c, align_bytes=ALIGN) for c in range(CHUNKS)]
+
+        def parts_of(c):
+            width = CHUNK // 2 if c == CHUNKS - 1 else CHUNK
+            return [slice(s0, s0 + width) for s0 in range(0, CHUNK, width)]
+
         for c in range(CHUNKS):
             copy = nc.vector.tensor_copy if c == VECTOR_BANK else nc.scalar.copy
-            copy(h_rounded[c][:], h_bank[c][:].rearrange("p t s -> p s t"))
+            for part in parts_of(c):
+                copy(h_rounded[c][:, part, :], h_bank[c][:, :, part].rearrange("p t s -> p s t"))
 
         def adapter(c):
-            nc.vector.quantize_mx(
-                out=h_codes[c][:].bitcast(FP8X4),
-                scales=h_plane[c][:],
-                in_=h_rounded[c][:].rearrange("p s t -> p (s t)"),
-            )
+            for part in parts_of(c):
+                nc.vector.quantize_mx(
+                    out=h_codes[c][:, part].bitcast(FP8X4),
+                    scales=h_plane[c][:, part],
+                    in_=h_rounded[c][:, part, :].rearrange("p s t -> p (s t)"),
+                )
             for m in range(M_TILES):
                 nc.tensor.matmul_mx(
                     out=out_part[c][m],

from contextlib import ExitStack

import concourse.mybir as mybir

K, T, S, H, N = 1024, 2048, 512, 512, 256
FLOPS = 2 * S * (K * H + K * N + H * N)

F32 = mybir.dt.float32
BF16 = mybir.dt.bfloat16
I32 = mybir.dt.int32
U32 = mybir.dt.uint32
U16 = mybir.dt.uint16
U8 = mybir.dt.uint8
FP8X4 = mybir.dt.float8_e4m3fn_x4
FP4X4 = mybir.dt.float4_e2m1fn_x4

P = 128
PACK = 4
K_PASS = P * PACK
PASSES = K // K_PASS
QUAD = 32
ROWS = 4
BLOCK_ROWS = QUAD // ROWS
PASS_STEP = BLOCK_ROWS // PASSES
CHUNK = 128
CHUNKS = S // CHUNK
GATHER = 256
M_TILES = N // P
ALIGN = 64
BURST = 256
SCALAR_SHARE = (64, 44)
VECTOR_BANK = 1


def tile_picked_phlora_none_p_kernel(
    tc, x_words, x_scales, w1_words, w1_scales, w2, w3_words, w3_scales, offs, out
):
    nc = tc.nc
    with ExitStack() as ctx:
        sb = ctx.enter_context(tc.tile_pool(name="sb", bufs=1))
        late = ctx.enter_context(tc.tile_pool(name="late", bufs=1))
        ps = ctx.enter_context(tc.psum_pool(name="ps", bufs=1))

        def words(ap):
            return ap.bitcast(I32)

        offsets = sb.tile([P, S // 16], U16, name="offsets")
        nc.sync.dma_start(offsets[:], offs)

        staged = sb.tile([P, S + 2 * N], U8, name="staged", align_bytes=ALIGN)
        nc.vector.memset(words(staged[:, S : S + N]), 0)
        byte_window = sb.tile([P, T], U8, name="byte_window", align_bytes=BURST)
        nc.vector.memset(words(byte_window[:]), 0)
        nc.sync.dma_start(words(staged[0:P:PASS_STEP, S : S + N]), words(w1_scales.rearrange("z q n -> q z n")))
        nc.sync.dma_start(words(byte_window[0:P:PASS_STEP, :]), words(x_scales.rearrange("z q c -> q z c")))

        lowered = sb.tile([P, S + 2 * N], U8, name="lowered", align_bytes=ALIGN)
        nc.vector.memset(words(lowered[:]), 0)
        raised = sb.tile([P, S], U8, name="raised", align_bytes=ALIGN)
        h_x_plane = [staged[:, 0:S], raised[PASS_STEP:P, :]]
        w1_x_plane = [staged[:, 0:S], lowered[:, 0:S]]
        w1_plane = [staged[:, S : S + N], lowered[:, S : S + N]]
        w3_plane = lowered[:, S + N : S + 2 * N]

        w2_raw = [sb.tile([P, PACK, H], F32, name="w2_raw%d" % z, align_bytes=BURST) for z in range(PASSES)]
        w2_rows = w2.rearrange("(z p j) c -> z p j c", z=PASSES, j=PACK)
        x_rows = x_words.rearrange("z p c r -> z p (c r)")
        nc.scalar.dma_start(w2_raw[0][:], w2_rows[0])
        word_window = [sb.tile([P, T], I32, name="word_window0", align_bytes=BURST)]
        nc.sync.dma_start(word_window[0][:], words(x_rows[0]))
        nc.sync.dma_start(w2_raw[1][:], w2_rows[1])

        picked_at = 4 * T
        w1_codes_at = 4 * T + S
        w3_codes_at = w1_codes_at + PASSES * 2 * N
        picked = late.tile([P, S], U8, name="picked", offset=picked_at, align_bytes=ALIGN)
        nc.vector.tensor_copy(picked[:], byte_window[:].indirect(offsets[:]))
        nc.vector.tensor_copy(words(staged[:, 0:S]), words(picked[:]))
        nc.vector.tensor_copy(words(raised[:]), words(picked[:]))
        for r in range(1, ROWS):
            nc.sync.dma_start(words(staged[r:P:QUAD, 0 : S + N]), words(staged[BLOCK_ROWS * r : P : QUAD, 0 : S + N]))

        word_window.append(late.tile([P, T], I32, name="word_window1", offset=0, align_bytes=BURST))
        nc.sync.dma_start(word_window[1][:], words(x_rows[1]))
        for r in range(1, ROWS):
            nc.sync.dma_start(
                words(raised[PASS_STEP + r : P : QUAD, :]), words(raised[PASS_STEP + BLOCK_ROWS * r : P : QUAD, :])
            )

        nc.sync.dma_start(words(staged[PASS_STEP:P:BLOCK_ROWS, S + N : S + 2 * N]), words(w3_scales[0]))
        w1_codes = late.tile([P, PASSES, 2 * N], U8, name="w1_codes", offset=w1_codes_at, align_bytes=ALIGN)
        nc.sync.dma_start(words(w1_codes[:]), words(w1_words.rearrange("z p n -> p z n")))
        w3_codes = late.tile([P, 2 * N], U8, name="w3_codes", offset=w3_codes_at, align_bytes=ALIGN)
        nc.sync.dma_start(words(w3_codes[:]), words(w3_words[0]))
        for r in range(ROWS):
            nc.sync.dma_start(words(lowered[r:P:QUAD, :]), words(staged[PASS_STEP + BLOCK_ROWS * r : P : QUAD, :]))

        w2_codes = [sb.tile([P, H], U32, name="w2_codes%d" % z, align_bytes=ALIGN) for z in range(PASSES)]
        w2_plane = [sb.tile([P, H], U8, name="w2_plane%d" % z, align_bytes=ALIGN) for z in range(PASSES)]
        x_codes = [sb.tile([P, S], U32, name="x_codes%d" % z, align_bytes=ALIGN) for z in range(PASSES)]
        h_bank = [ps.tile([P, PACK, CHUNK], F32, name="h_bank%d" % c) for c in range(CHUNKS)]

        def quantise_w2(z):
            grouped = sb.tile([P, PACK, P, PACK], BF16, name="w2_grouped%d" % z, align_bytes=ALIGN)
            share = SCALAR_SHARE[z]
            for copy, m0, m1 in ((nc.scalar.copy, 0, share), (nc.vector.tensor_copy, share, P)):
                copy(
                    grouped[:, :, m0:m1, :].rearrange("p t m j -> p m j t"),
                    w2_raw[z][:].rearrange("p j (m t) -> p m j t", t=PACK)[:, m0:m1, :, :],
                )
            nc.vector.quantize_mx(
                out=w2_codes[z][:].bitcast(FP8X4),
                scales=w2_plane[z][:],
                in_=grouped[:].rearrange("p t m j -> p (t m j)"),
            )

        def gather_words(z):
            for g in range(S // GATHER):
                nc.vector.tensor_copy(
                    x_codes[z][:, g * GATHER : (g + 1) * GATHER],
                    word_window[z][:].bitcast(U32).indirect(offsets[:, g * GATHER // 16 : (g + 1) * GATHER // 16]),
                )

        def x_operand(z, c0, c1, x_plane):
            places = slice(c0 * CHUNK, c1 * CHUNK)
            return x_codes[z][:, places].bitcast(FP8X4), x_plane[z][:, places]

        def h_passes(z, c):
            rhs, rhs_scale = x_operand(z, c, c + 1, h_x_plane)
            for t in range(PACK):
                nc.tensor.matmul_mx(
                    out=h_bank[c][:, t, :],
                    lhsT=w2_codes[z][:, t * P : (t + 1) * P].bitcast(FP8X4),
                    lhsT_scale=w2_plane[z][:, t * P : (t + 1) * P],
                    rhs=rhs,
                    rhs_scale=rhs_scale,
                    start=(z == 0 and t == 0),
                    stop=(z == PASSES - 1 and t == PACK - 1),
                )

        first_bank = ps.tile([P, M_TILES, CHUNK], F32, name="first_bank")
        middle_banks = [ps.tile([P, 2 * CHUNK], F32, name="middle_bank%d" % m) for m in range(M_TILES)]
        out_part = [[first_bank[:, m, :] for m in range(M_TILES)]]
        out_part.extend([bank[:, u * CHUNK : (u + 1) * CHUNK] for bank in middle_banks] for u in range(2))
        closes_bank = ((False, True), (False, False), (True, True), (True, True))

        def w1_passes(parts, c0, c1, z, opens):
            rhs, rhs_scale = x_operand(z, c0, c1, w1_x_plane)
            for m in range(M_TILES):
                nc.tensor.matmul_mx(
                    out=parts[m],
                    lhsT=w1_codes[:, z, 2 * m * P : 2 * (m + 1) * P].bitcast(FP4X4),
                    lhsT_scale=w1_plane[z][:, m * P : (m + 1) * P],
                    rhs=rhs,
                    rhs_scale=rhs_scale,
                    start=(opens and (m == 0 or c0 > 0)),
                    stop=False,
                )

        middle_part = [bank[:] for bank in middle_banks]
        for z in range(PASSES):
            quantise_w2(z)
            gather_words(z)
            for c in range(CHUNKS):
                h_passes(z, c)

        h_codes = [sb.tile([P, CHUNK], U32, name="h_codes%d" % c, align_bytes=ALIGN) for c in range(CHUNKS)]
        h_plane = [sb.tile([P, CHUNK], U8, name="h_plane%d" % c, align_bytes=ALIGN) for c in range(CHUNKS)]
        h_rounded = [sb.tile([P, CHUNK, PACK], BF16, name="h_rounded%d" % c, align_bytes=ALIGN) for c in range(CHUNKS)]

        def parts_of(c):
            width = CHUNK // 2 if c == CHUNKS - 1 else CHUNK
            return [slice(s0, s0 + width) for s0 in range(0, CHUNK, width)]

        for c in range(CHUNKS):
            copy = nc.vector.tensor_copy if c == VECTOR_BANK else nc.scalar.copy
            for part in parts_of(c):
                copy(h_rounded[c][:, part, :], h_bank[c][:, :, part].rearrange("p t s -> p s t"))

        def adapter(c):
            for part in parts_of(c):
                nc.vector.quantize_mx(
                    out=h_codes[c][:, part].bitcast(FP8X4),
                    scales=h_plane[c][:, part],
                    in_=h_rounded[c][:, part, :].rearrange("p s t -> p (s t)"),
                )
            for m in range(M_TILES):
                nc.tensor.matmul_mx(
                    out=out_part[c][m],
                    lhsT=w3_codes[:, 2 * m * P : 2 * (m + 1) * P].bitcast(FP4X4),
                    lhsT_scale=w3_plane[:, m * P : (m + 1) * P],
                    rhs=h_codes[c][:].bitcast(FP8X4),
                    rhs_scale=h_plane[c][:],
                    start=False,
                    stop=closes_bank[c][m],
                )

        last_banks = [ps.tile([P, CHUNK], F32, name=name) for name in ("last_bank", "h_bank0")]
        out_part.append([bank[:] for bank in last_banks])
        w1_passes(out_part[0], 0, 1, 0, True)
        w1_passes(middle_part, 1, 3, 0, True)
        w1_passes(out_part[0], 0, 1, 1, False)
        adapter(0)
        w1_passes(middle_part, 1, 3, 1, False)
        adapter(1)
        adapter(2)
        w1_passes(out_part[3], 3, 4, 1, True)
        w1_passes(out_part[3], 3, 4, 0, False)
        adapter(3)

        copies = (nc.vector.tensor_copy, nc.scalar.copy)
        out_rows = out.rearrange("(m p) s -> p m s", p=P)
        first = sb.tile([P, M_TILES, CHUNK], F32, name="first_result", align_bytes=BURST)
        nc.scalar.copy(first[:], first_bank[:])
        nc.sync.dma_start(out_rows[:, :, 0:CHUNK], first[:])
        middle = sb.tile([P, M_TILES, 2 * CHUNK], F32, name="middle_result", align_bytes=BURST)
        for m in range(M_TILES):
            copies[m](middle[:, m, :], middle_banks[m][:])
        nc.sync.dma_start(out_rows[:, :, CHUNK : 3 * CHUNK], middle[:])
        for m in range(M_TILES):
            last = sb.tile([P, CHUNK], F32, name="last_result%d" % m, align_bytes=BURST)
            copies[m](last[:], last_banks[m][:])
            nc.sync.dma_start(out_rows[:, m, S - CHUNK : S], last[:])
